import numpy as np
import ml_dtypes


def mxq(x, axis, fmt="e4m3"):
    dtype, down = {"e4m3": (ml_dtypes.float8_e4m3fn, 7), "e5m2": (ml_dtypes.float8_e5m2, 14)}[fmt]
    v = np.moveaxis(np.asarray(x, np.float32).astype(ml_dtypes.bfloat16).astype(np.float64), axis, -1)
    blocks = v.reshape(v.shape[:-1] + (-1, 32))
    amax = np.abs(blocks).max(-1, keepdims=True)
    byte = np.maximum(np.where(amax > 0, np.frexp(amax)[1] - 1 + 127, 0) - down, 1)
    scale = np.exp2(byte - 127.0)
    codes = (blocks / scale).astype(np.float32).astype(dtype).astype(np.float64)
    return np.moveaxis((codes * scale).reshape(v.shape), -1, axis)


WIDE = False


def mx_kscale(k):
    if not WIDE:
        return np.ones(k)
    levels = np.array([10, -10, 5, -5, 0])
    if k % 512:
        return np.exp2(np.random.permutation(np.resize(levels, k // 32))).repeat(32)
    a = np.empty((k // 512, 16))
    for p in range(k // 512):
        a[p, :8] = np.random.permutation(np.resize(levels, 8))
        for g in range(8):
            far = levels[np.abs(levels - a[p, g]) >= 10]
            a[p, g + 8] = far[np.random.randint(len(far))]
    return np.exp2(a.ravel()).repeat(32)


def f64(x):
    return np.asarray(x).astype(np.float64)


def striped(idx):
    return np.tile(np.asarray(idx).reshape(-1, 16).T, (8, 1)).astype(np.uint16)


def unstriped(offs):
    return offs[:16].T.reshape(-1).astype(np.int64)


E2M1 = np.array([0.0, 0.5, 1.0, 1.5, 2.0, 3.0, 4.0, 6.0, -0.0, -0.5, -1.0, -1.5, -2.0, -3.0, -4.0, -6.0])


def pack_weight(w, fmt):
    k, n = w.shape
    w = f64(np.asarray(w, np.float32).astype(ml_dtypes.bfloat16)).reshape(k // 32, 32, n)
    amax = np.abs(w).max(1)
    if fmt == "e4m3":
        byte = np.frexp(amax)[1] - 1 + 127 - 7
    else:
        mant, ex = np.frexp(amax / 6.0)
        byte = np.where(mant > 0.5, ex, ex - 1) + 127
    byte = np.clip(np.where(amax > 0, byte, 1), 1, 254)
    scaled = (w * np.exp2(127.0 - byte)[:, None, :]).reshape(k, n).astype(np.float32)
    by_word = np.ascontiguousarray(scaled.reshape(k // 512, 128, 4, n).transpose(0, 1, 3, 2))
    if fmt == "e4m3":
        words = by_word.astype(ml_dtypes.float8_e4m3fn).view(np.uint8)
    else:
        c = by_word.astype(ml_dtypes.float4_e2m1fn).view(np.uint8) & 0xF
        words = (c[..., 0::2] | (c[..., 1::2] << 4)).reshape(k // 512, 128, 2 * n)
    return np.ascontiguousarray(words), np.ascontiguousarray(byte.astype(np.uint8).reshape(k // 512, 16, n))


def unpack_weight(words, scales, fmt):
    g, _, n = scales.shape
    words = np.ascontiguousarray(words).reshape(g, 128, n, -1)
    if fmt == "e4m3":
        vals = words.view(ml_dtypes.float8_e4m3fn).astype(np.float64)
    else:
        nib = np.empty((g, 128, n, 4), np.uint8)
        nib[..., 0::2] = words & 0xF
        nib[..., 1::2] = words >> 4
        vals = E2M1[nib]
    vals = vals * np.repeat(np.exp2(scales.astype(np.float64) - 127.0), 8, axis=1)[..., None]
    return vals.transpose(0, 1, 3, 2).reshape(g * 512, n)


def rot(x):
    y = x.reshape(-1, 2, x.shape[1])
    return np.stack([-y[:, 1], y[:, 0]], axis=1).reshape(x.shape)


C, D, R, T, I, U, Q = 512, 512, 512, 2048, 512, 1024, 128


def setup_inputs():
    n = np.random.standard_normal
    idx = np.random.permutation(T)[:I]
    idx2 = np.random.randint(0, U, I)
    fc = mx_kscale(C)
    fd = mx_kscale(D)
    fr = mx_kscale(R)
    latp = pack_weight(n((C, T)) / fc[:, None], "e4m3")
    return {
        "lat_words": latp[0],
        "lat_scales": latp[1],
        "wuk": (n((C, D)) * 1 / np.sqrt(C) * fc[:, None] / fd).astype(np.float32),
        "query": (n((D, Q)) * 0.3 / np.sqrt(D) * fd[:, None]).astype(np.float32),
        "krot": (n((R, T)) / fr[:, None]).astype(np.float32),
        "cosn": (np.repeat(np.round(np.cos(np.arange(R // 2)[:, None] * 0.11 + np.arange(U)[None] * 0.37) * 64) / 64, 2, axis=0)).astype(np.float32),
        "sinn": (np.repeat(np.round(np.sin(np.arange(R // 2)[:, None] * 0.11 + np.arange(U)[None] * 0.37) * 64) / 64, 2, axis=0)).astype(np.float32),
        "qrot": (n((R, Q)) * 0.3 / np.sqrt(R) * fr[:, None]).astype(np.float32),
        "offs": striped(idx),
        "offs2": striped(idx2),
    }


def reference(lat_words, lat_scales, wuk, query, krot, cosn, sinn, qrot, offs, offs2):
    idx = unstriped(offs)
    idx2 = unstriped(offs2)
    latu = unpack_weight(lat_words, lat_scales, "e4m3")
    wukq = mxq(f64(wuk), 0, "e4m3")
    latidxg = latu[:, idx]
    b = wukq.T @ latidxg
    kr = rot(f64(krot)[:, idx])
    km = f64(krot)[:, idx] * f64(cosn)[:, idx2] + kr * f64(sinn)[:, idx2]
    queryq = mxq(f64(query), 0, "e4m3")
    bq = mxq(b, 0, "e4m3")
    qrotq = mxq(f64(qrot), 0, "e4m3")
    kmq = mxq(km, 0, "e4m3")
    a = queryq.T @ bq + qrotq.T @ kmq
    p = np.exp(a - np.max(a, axis=1, keepdims=True))
    y = p / np.sum(p, axis=1, keepdims=True) * 512.0
    return y

@@ -1,0 +1,197 @@
+from contextlib import ExitStack
+
+import concourse.mybir as mybir
+
+C, D, R, T, I, U, Q = 512, 512, 512, 2048, 512, 1024, 128
+FLOPS = 2 * C * D * I + 2 * (D + R) * Q * I
+
+F32 = mybir.dt.float32
+BF16 = mybir.dt.bfloat16
+I32 = mybir.dt.int32
+U32 = mybir.dt.uint32
+U16 = mybir.dt.uint16
+U8 = mybir.dt.uint8
+FP8X4 = mybir.dt.float8_e4m3fn_x4
+ALU = mybir.AluOpType
+ACT = mybir.ActivationFunctionType
+AXIS = mybir.AxisListType
+
+P = 128
+PACK = 4
+CHUNK = 128
+HALF = I // 2
+RUN = 4
+
+
+def tile_attend_mla_expand_kernel(tc, lat_words, lat_scales, wuk, query, krot, cosn, sinn, qrot, offs, offs2, out):
+    nc = tc.nc
+    with ExitStack() as ctx:
+        sb = ctx.enter_context(tc.tile_pool(name="sb", bufs=1))
+        ps = ctx.enter_context(tc.psum_pool(name="ps", bufs=1))
+
+        tokens = sb.tile([P, I // 16], U16, name="tokens")
+        places = sb.tile([P, I // 16], U16, name="places")
+        k_rows = krot.rearrange("(p t) n -> p t n", t=PACK)
+        c_rows = cosn.rearrange("(p t) n -> p t n", t=PACK)
+        s_rows = sinn.rearrange("(p t) n -> p t n", t=PACK)
+        k_pool = [sb.tile([P, T], F32, name=f"k_pool{t}") for t in range(PACK)]
+        c_pool = [sb.tile([P, U], F32, name=f"c_pool{u}") for u in range(2)]
+        s_pool = [sb.tile([P, U], F32, name=f"s_pool{u}") for u in range(2)]
+        word_pool = sb.tile([P, T], I32, name="word_pool")
+        byte_pool = sb.tile([P, T], U8, name="byte_pool")
+        w_raw = sb.tile([P, PACK, D], F32, name="w_raw")
+        q_raw = sb.tile([P, PACK, Q], F32, name="q_raw")
+        qr_raw = sb.tile([P, PACK, Q], F32, name="qr_raw")
+
+        warm_in = sb.tile([P, 1], F32, name="warm_in")
+        warm_out = sb.tile([P, 1], F32, name="warm_out")
+        nc.vector.memset(warm_in[:], 0.0)
+        nc.scalar.activation(warm_out[:], warm_in[:], ACT.Exp)
+
+        nc.vector.memset(byte_pool[:].bitcast(I32), 0)
+        nc.sync.dma_start(tokens[:], offs)
+        for g in range(4):
+            nc.scalar.dma_start(
+                byte_pool[32 * g : 32 * g + 4, :].bitcast(I32),
+                lat_scales[0, 4 * g : 4 * g + 4, :].bitcast(I32),
+            )
+        nc.sync.dma_start(c_pool[0][:], c_rows[:, 0, :])
+        nc.sync.dma_start(places[:], offs2)
+        nc.sync.dma_start(s_pool[0][:], s_rows[:, 0, :])
+        nc.sync.dma_start(k_pool[0][:], k_rows[:, 0, :])
+        nc.sync.dma_start(k_pool[1][:], k_rows[:, 1, :])
+        nc.sync.dma_start(w_raw[:], wuk.rearrange("(p j) d -> p j d", j=PACK))
+        nc.sync.dma_start(word_pool[:], lat_words[0].rearrange("p n t -> p (n t)").bitcast(I32))
+        nc.sync.dma_start(c_pool[1][:], c_rows[:, 2, :])
+        nc.sync.dma_start(s_pool[1][:], s_rows[:, 2, :])
+        nc.sync.dma_start(k_pool[2][:], k_rows[:, 2, :])
+        nc.sync.dma_start(k_pool[3][:], k_rows[:, 3, :])
+        nc.sync.dma_start(q_raw[:], query.rearrange("(p j) q -> p j q", j=PACK))
+        nc.sync.dma_start(qr_raw[:], qrot.rearrange("(p j) q -> p j q", j=PACK))
+
+        def quantise(name, grouped, width):
+            codes = sb.tile([P, width], U32, name=f"{name}_codes", align_bytes=64)
+            scales = sb.tile([P, width], U8, name=f"{name}_scales", align_bytes=64)
+            nc.vector.quantize_mx(out=codes[:].bitcast(FP8X4), scales=scales[:], in_=grouped)
+            return codes, scales
+
+        lat_bytes = sb.tile([P, I], U8, name="lat_bytes", align_bytes=64)
+        nc.vector.tensor_copy(lat_bytes[:], byte_pool[:].indirect(tokens[:]))
+
+        pairs = sb.tile([P, 2, I, 2], BF16, name="pairs")
+
+        def factors(u):
+            trig = sb.tile([P, 3, I], F32, name=f"trig{u}")
+            nc.vector.tensor_copy(trig[:, 1, :], c_pool[u][:].indirect(places[:]))
+            nc.vector.tensor_copy(trig[:, 2, :], s_pool[u][:].indirect(places[:]))
+            nc.scalar.activation(trig[:, 0, :], trig[:, 2, :], ACT.Copy, scale=-1.0)
+            return trig
+
+        def products(t, factor_pair, cols, tag):
+            n = cols.stop - cols.start
+            keys = sb.tile([P, n], F32, name=f"keys{t}{tag}")
+            nc.vector.tensor_copy(keys[:], k_pool[t][:].indirect(tokens[:, cols.start // 16 : cols.stop // 16]))
+            prod = sb.tile([P, 2, n], F32, name=f"prod{t}{tag}")
+            nc.vector.tensor_tensor(
+                prod[:], keys[:].unsqueeze(1).to_broadcast([P, 2, n]), factor_pair[:, :, cols], ALU.mult
+            )
+            return prod
+
+        def rotate(u, even, odd, cols):
+            nc.vector.tensor_tensor(
+                pairs[:, u, cols, :].rearrange("p (c i) e -> p c e i", i=RUN),
+                even.rearrange("p e (c i) -> p c e i", i=RUN),
+                odd.rearrange("p e (c i) -> p c e i", i=RUN),
+                ALU.add,
+            )
+
+        whole = slice(0, I)
+        trig0 = factors(0)
+        prod0 = products(0, trig0[:, 1:3, :], whole, "")
+        prod1 = products(1, trig0[:, 0:2, :], whole, "")
+        rotate(0, prod0[:], prod1[:], whole)
+
+        w_grouped = sb.tile([P, PACK, P, PACK], BF16, name="w_grouped", align_bytes=64)
+        nc.scalar.copy(
+            w_grouped[:].rearrange("p t m j -> p m j t"),
+            w_raw[:].rearrange("p j (m t) -> p m j t", t=PACK),
+        )
+        w_codes, w_scales = quantise("w", w_grouped[:].rearrange("p t m j -> p (t m j)"), D)
+
+        lat_codes = sb.tile([P, I], U32, name="lat_codes", align_bytes=64)
+        nc.vector.tensor_copy(lat_codes[:], word_pool[:].bitcast(U32).indirect(tokens[:]))
+
+        b_grouped = sb.tile([P, I, PACK], BF16, name="b_grouped", align_bytes=64)
+        for n in range(I // CHUNK):
+            cols = slice(n * CHUNK, (n + 1) * CHUNK)
+            bank = ps.tile([P, PACK, CHUNK], F32, name=f"b_bank{n}")
+            for t in range(PACK):
+                rows = slice(t * P, (t + 1) * P)
+                nc.tensor.matmul_mx(
+                    out=bank[:, t, :],
+                    lhsT=w_codes[:, rows].bitcast(FP8X4),
+                    lhsT_scale=w_scales[:, rows],
+                    rhs=lat_codes[:, cols].bitcast(FP8X4),
+                    rhs_scale=lat_bytes[:, cols],
+                    start=True,
+                    stop=True,
+                )
+            nc.scalar.copy(b_grouped[:, cols, :], bank[:].rearrange("p t i -> p i t"))
+
+        trig1 = factors(1)
+        b_codes, b_scales = quantise("b", b_grouped[:].rearrange("p i t -> p (i t)"), I)
+        prod2 = products(2, trig1[:, 1:3, :], whole, "")
+
+        def stationary(name, raw):
+            grouped = sb.tile([P, Q, PACK], BF16, name=f"{name}_grouped", align_bytes=64)
+            nc.scalar.copy(
+                grouped[:].rearrange("p (c i) j -> p c j i", i=RUN),
+                raw[:].rearrange("p j (c i) -> p c j i", i=RUN),
+            )
+            return quantise(name, grouped[:].rearrange("p q j -> p (q j)"), Q)
+
+        halves = [slice(h * HALF, (h + 1) * HALF) for h in range(2)]
+        prod3 = [products(3, trig1[:, 0:2, :], cols, f"h{h}") for h, cols in enumerate(halves)]
+        for h, cols in enumerate(halves):
+            rotate(1, prod2[:, :, cols], prod3[h][:], cols)
+        km_grouped = [sb.tile([P, HALF, PACK], BF16, name=f"km_grouped{h}", align_bytes=64) for h in range(2)]
+        pair_words = pairs[:].rearrange("p u i e -> p u (i e)").bitcast(F32)
+        for h, cols in enumerate(halves):
+            nc.scalar.copy(
+                km_grouped[h][:].rearrange("p i t -> p (i t)").bitcast(F32).rearrange("p (c i u) -> p c u i", i=RUN, u=2),
+                pair_words[:, :, cols].rearrange("p u (c i) -> p c u i", i=RUN),
+            )
+        q_codes, q_scales = stationary("q", q_raw)
+        qr_codes, qr_scales = stationary("qr", qr_raw)
+
+        scores = ps.tile([P, I], F32, name="scores")
+        for h, cols in enumerate(halves):
+            km_codes, km_scales = quantise(f"km{h}", km_grouped[h][:].rearrange("p i t -> p (i t)"), HALF)
+            nc.tensor.matmul_mx(
+                out=scores[:, cols],
+                lhsT=q_codes[:].bitcast(FP8X4),
+                lhsT_scale=q_scales[:],
+                rhs=b_codes[:, cols].bitcast(FP8X4),
+                rhs_scale=b_scales[:, cols],
+                start=True,
+                stop=False,
+            )
+            nc.tensor.matmul_mx(
+                out=scores[:, cols],
+                lhsT=qr_codes[:].bitcast(FP8X4),
+                lhsT_scale=qr_scales[:],
+                rhs=km_codes[:].bitcast(FP8X4),
+                rhs_scale=km_scales[:],
+                start=False,
+                stop=True,
+            )
+        shift = sb.tile([P, 1], F32, name="shift")
+        nc.vector.tensor_reduce(shift[:], scores[:], AXIS.X, ALU.max, negate=True)
+        weights = sb.tile([P, I], F32, name="weights")
+        total = sb.tile([P, 1], F32, name="total")
+        nc.scalar.activation(weights[:], scores[:], ACT.Exp, bias=shift[:], accum_out=total[:])
+        inverse = sb.tile([P, 1], F32, name="inverse")
+        nc.vector.reciprocal(inverse[:], total[:])
+        result = sb.tile([P, I], F32, name="result")
+        nc.vector.tensor_scalar(result[:], weights[:], inverse[:], float(I), ALU.mult, ALU.mult)
+        nc.sync.dma_start(out, result[:])

@@ -55,12 +55,12 @@ def tile_attend_mla_expand_kernel(tc, lat_words, lat_scales, wuk, query, krot, c
                 byte_pool[32 * g : 32 * g + 4, :].bitcast(I32),
                 lat_scales[0, 4 * g : 4 * g + 4, :].bitcast(I32),
             )
+        nc.sync.dma_start(w_raw[:], wuk.rearrange("(p j) d -> p j d", j=PACK))
         nc.sync.dma_start(c_pool[0][:], c_rows[:, 0, :])
         nc.sync.dma_start(places[:], offs2)
         nc.sync.dma_start(s_pool[0][:], s_rows[:, 0, :])
         nc.sync.dma_start(k_pool[0][:], k_rows[:, 0, :])
         nc.sync.dma_start(k_pool[1][:], k_rows[:, 1, :])
-        nc.sync.dma_start(w_raw[:], wuk.rearrange("(p j) d -> p j d", j=PACK))
         nc.sync.dma_start(word_pool[:], lat_words[0].rearrange("p n t -> p (n t)").bitcast(I32))
         nc.sync.dma_start(c_pool[1][:], c_rows[:, 2, :])
         nc.sync.dma_start(s_pool[1][:], s_rows[:, 2, :])
@@ -78,7 +78,6 @@ def tile_attend_mla_expand_kernel(tc, lat_words, lat_scales, wuk, query, krot, c
         lat_bytes = sb.tile([P, I], U8, name="lat_bytes", align_bytes=64)
         nc.vector.tensor_copy(lat_bytes[:], byte_pool[:].indirect(tokens[:]))
 
-        pairs = sb.tile([P, 2, I, 2], BF16, name="pairs")
 
         def factors(u):
             trig = sb.tile([P, 3, I], F32, name=f"trig{u}")
@@ -106,17 +105,30 @@ def tile_attend_mla_expand_kernel(tc, lat_words, lat_scales, wuk, query, krot, c
             )
 
         whole = slice(0, I)
-        trig0 = factors(0)
-        prod0 = products(0, trig0[:, 1:3, :], whole, "")
-        prod1 = products(1, trig0[:, 0:2, :], whole, "")
-        rotate(0, prod0[:], prod1[:], whole)
-
         w_grouped = sb.tile([P, PACK, P, PACK], BF16, name="w_grouped", align_bytes=64)
-        nc.scalar.copy(
-            w_grouped[:].rearrange("p t m j -> p m j t"),
-            w_raw[:].rearrange("p j (m t) -> p m j t", t=PACK),
-        )
+        for u in range(2):
+            nc.scalar.copy(
+                w_grouped[:, 2 * u : 2 * u + 2].rearrange("p t m j -> p m j t"),
+                w_raw[:].rearrange("p j (m t) -> p m j t", t=PACK)[:, :, :, 2 * u : 2 * u + 2],
+            )
         w_codes, w_scales = quantise("w", w_grouped[:].rearrange("p t m j -> p (t m j)"), D)
+
+        cos0 = sb.tile([P, I], F32, name="cos0")
+        sin0 = sb.tile([P, I], F32, name="sin0")
+        nc.vector.tensor_copy(cos0[:], c_pool[0][:].indirect(places[:]))
+        nc.vector.tensor_copy(sin0[:], s_pool[0][:].indirect(places[:]))
+        terms = []
+        for t in range(2):
+            keys = sb.tile([P, I], F32, name=f"keys{t}")
+            nc.vector.tensor_copy(keys[:], k_pool[t][:].indirect(tokens[:]))
+            by_cos = sb.tile([P, I], F32, name=f"by_cos{t}")
+            by_sin = sb.tile([P, I], F32, name=f"by_sin{t}")
+            nc.gpsimd.tensor_tensor(by_cos[:], keys[:], cos0[:], ALU.mult)
+            nc.gpsimd.tensor_tensor(by_sin[:], keys[:], sin0[:], ALU.mult)
+            terms.append((by_cos, by_sin))
+        planes = sb.tile([P, 2, I], BF16, name="planes")
+        nc.gpsimd.tensor_tensor(planes[:, 0, :], terms[0][0][:], terms[1][1][:], ALU.subtract)
+        nc.gpsimd.tensor_tensor(planes[:, 1, :], terms[1][0][:], terms[0][1][:], ALU.add)
 
         lat_codes = sb.tile([P, I], U32, name="lat_codes", align_bytes=64)
         nc.vector.tensor_copy(lat_codes[:], word_pool[:].bitcast(U32).indirect(tokens[:]))
@@ -139,6 +151,11 @@ def tile_attend_mla_expand_kernel(tc, lat_words, lat_scales, wuk, query, krot, c
             nc.scalar.copy(b_grouped[:, cols, :], bank[:].rearrange("p t i -> p i t"))
 
         trig1 = factors(1)
+        pairs = sb.tile([P, 2, I, 2], BF16, name="pairs", tag="lat_codes", align_bytes=64)
+        nc.scalar.copy(
+            pairs[:, 0].rearrange("p (c i) e -> p c e i", i=RUN),
+            planes[:].rearrange("p e (c i) -> p c e i", i=RUN),
+        )
         b_codes, b_scales = quantise("b", b_grouped[:].rearrange("p i t -> p (i t)"), I)
         prod2 = products(2, trig1[:, 1:3, :], whole, "")
 

@@ -45,21 +45,32 @@ def tile_attend_mla_expand_kernel(tc, lat_words, lat_scales, wuk, query, krot, c
 
         warm_in = sb.tile([P, 1], F32, name="warm_in")
         warm_out = sb.tile([P, 1], F32, name="warm_out")
+        nc.vector.memset(byte_pool[:].bitcast(I32), 0)
         nc.vector.memset(warm_in[:], 0.0)
         nc.scalar.activation(warm_out[:], warm_in[:], ACT.Exp)
 
-        nc.vector.memset(byte_pool[:].bitcast(I32), 0)
-        nc.sync.dma_start(tokens[:], offs)
-        for g in range(4):
-            nc.scalar.dma_start(
-                byte_pool[32 * g : 32 * g + 4, :].bitcast(I32),
-                lat_scales[0, 4 * g : 4 * g + 4, :].bitcast(I32),
-            )
         nc.sync.dma_start(w_raw[:], wuk.rearrange("(p j) d -> p j d", j=PACK))
+        for g in range(2):
+            nc.sync.dma_start(
+                byte_pool[64 * g : 64 * g + 32 : 4, :].bitcast(I32),
+                lat_scales[0, 8 * g : 8 * g + 8, :].bitcast(I32),
+            )
+        nc.sync.dma_start(tokens[:], offs)
         nc.sync.dma_start(c_pool[0][:], c_rows[:, 0, :])
         nc.sync.dma_start(places[:], offs2)
         nc.sync.dma_start(s_pool[0][:], s_rows[:, 0, :])
         nc.sync.dma_start(k_pool[0][:], k_rows[:, 0, :])
+        picked_bytes = sb.tile([P, I], U8, name="picked_bytes")
+        nc.vector.tensor_copy(picked_bytes[:], byte_pool[:].indirect(tokens[:]))
+        lat_bytes = sb.tile([P, I], U8, name="lat_bytes", align_bytes=64)
+        nc.vector.memset(lat_bytes[:].bitcast(I32), 0)
+        for g in range(4):
+            first = 64 * (g // 2) + 16 * (g % 2)
+            nc.sync.dma_start(
+                lat_bytes[32 * g : 32 * g + 4, :].bitcast(I32),
+                picked_bytes[first : first + 16 : 4, :].bitcast(I32),
+            )
+
         nc.sync.dma_start(k_pool[1][:], k_rows[:, 1, :])
         nc.sync.dma_start(word_pool[:], lat_words[0].rearrange("p n t -> p (n t)").bitcast(I32))
         nc.sync.dma_start(c_pool[1][:], c_rows[:, 2, :])
@@ -74,10 +85,6 @@ def tile_attend_mla_expand_kernel(tc, lat_words, lat_scales, wuk, query, krot, c
             scales = sb.tile([P, width], U8, name=f"{name}_scales", align_bytes=64)
             nc.vector.quantize_mx(out=codes[:].bitcast(FP8X4), scales=scales[:], in_=grouped)
             return codes, scales
-
-        lat_bytes = sb.tile([P, I], U8, name="lat_bytes", align_bytes=64)
-        nc.vector.tensor_copy(lat_bytes[:], byte_pool[:].indirect(tokens[:]))
-
 
         def factors(u):
             trig = sb.tile([P, 3, I], F32, name=f"trig{u}")
@@ -159,14 +166,6 @@ def tile_attend_mla_expand_kernel(tc, lat_words, lat_scales, wuk, query, krot, c
         b_codes, b_scales = quantise("b", b_grouped[:].rearrange("p i t -> p (i t)"), I)
         prod2 = products(2, trig1[:, 1:3, :], whole, "")
 
-        def stationary(name, raw):
-            grouped = sb.tile([P, Q, PACK], BF16, name=f"{name}_grouped", align_bytes=64)
-            nc.scalar.copy(
-                grouped[:].rearrange("p (c i) j -> p c j i", i=RUN),
-                raw[:].rearrange("p j (c i) -> p c j i", i=RUN),
-            )
-            return quantise(name, grouped[:].rearrange("p q j -> p (q j)"), Q)
-
         halves = [slice(h * HALF, (h + 1) * HALF) for h in range(2)]
         prod3 = [products(3, trig1[:, 0:2, :], cols, f"h{h}") for h, cols in enumerate(halves)]
         for h, cols in enumerate(halves):
@@ -178,16 +177,21 @@ def tile_attend_mla_expand_kernel(tc, lat_words, lat_scales, wuk, query, krot, c
                 km_grouped[h][:].rearrange("p i t -> p (i t)").bitcast(F32).rearrange("p (c i u) -> p c u i", i=RUN, u=2),
                 pair_words[:, :, cols].rearrange("p u (c i) -> p c u i", i=RUN),
             )
-        q_codes, q_scales = stationary("q", q_raw)
-        qr_codes, qr_scales = stationary("qr", qr_raw)
+        q_grouped = sb.tile([P, 2, Q, PACK], BF16, name="q_grouped", align_bytes=64)
+        for n, raw in enumerate((q_raw, qr_raw)):
+            nc.scalar.copy(
+                q_grouped[:, n].rearrange("p (c i) j -> p c j i", i=RUN),
+                raw[:].rearrange("p j (c i) -> p c j i", i=RUN),
+            )
+        q_codes, q_scales = quantise("q", q_grouped[:].rearrange("p n q j -> p (n q j)"), 2 * Q)
 
         scores = ps.tile([P, I], F32, name="scores")
         for h, cols in enumerate(halves):
             km_codes, km_scales = quantise(f"km{h}", km_grouped[h][:].rearrange("p i t -> p (i t)"), HALF)
             nc.tensor.matmul_mx(
                 out=scores[:, cols],
-                lhsT=q_codes[:].bitcast(FP8X4),
-                lhsT_scale=q_scales[:],
+                lhsT=q_codes[:, :Q].bitcast(FP8X4),
+                lhsT_scale=q_scales[:, :Q],
                 rhs=b_codes[:, cols].bitcast(FP8X4),
                 rhs_scale=b_scales[:, cols],
                 start=True,
@@ -195,8 +199,8 @@ def tile_attend_mla_expand_kernel(tc, lat_words, lat_scales, wuk, query, krot, c
             )
             nc.tensor.matmul_mx(
                 out=scores[:, cols],
-                lhsT=qr_codes[:].bitcast(FP8X4),
-                lhsT_scale=qr_scales[:],
+                lhsT=q_codes[:, Q:].bitcast(FP8X4),
+                lhsT_scale=q_scales[:, Q:],
                 rhs=km_codes[:].bitcast(FP8X4),
                 rhs_scale=km_scales[:],
                 start=False,

@@ -185,11 +185,11 @@ def tile_attend_mla_expand_kernel(tc, lat_words, lat_scales, wuk, query, krot, c
             )
         q_codes, q_scales = quantise("q", q_grouped[:].rearrange("p n q j -> p (n q j)"), 2 * Q)
 
-        scores = ps.tile([P, I], F32, name="scores")
+        scores = [ps.tile([P, HALF], F32, name=f"scores{h}") for h in range(2)]
         for h, cols in enumerate(halves):
             km_codes, km_scales = quantise(f"km{h}", km_grouped[h][:].rearrange("p i t -> p (i t)"), HALF)
             nc.tensor.matmul_mx(
-                out=scores[:, cols],
+                out=scores[h][:],
                 lhsT=q_codes[:, :Q].bitcast(FP8X4),
                 lhsT_scale=q_scales[:, :Q],
                 rhs=b_codes[:, cols].bitcast(FP8X4),
@@ -198,7 +198,7 @@ def tile_attend_mla_expand_kernel(tc, lat_words, lat_scales, wuk, query, krot, c
                 stop=False,
             )
             nc.tensor.matmul_mx(
-                out=scores[:, cols],
+                out=scores[h][:],
                 lhsT=q_codes[:, Q:].bitcast(FP8X4),
                 lhsT_scale=q_scales[:, Q:],
                 rhs=km_codes[:].bitcast(FP8X4),
@@ -206,13 +206,20 @@ def tile_attend_mla_expand_kernel(tc, lat_words, lat_scales, wuk, query, krot, c
                 start=False,
                 stop=True,
             )
-        shift = sb.tile([P, 1], F32, name="shift")
-        nc.vector.tensor_reduce(shift[:], scores[:], AXIS.X, ALU.max, negate=True)
+        negated = sb.tile([P, I], F32, name="negated")
+        shifts = [sb.tile([P, 1], F32, name=f"shift{h}") for h in range(2)]
+        nc.vector.tensor_scalar(
+            negated[:, halves[0]], scores[0][:], -1.0, None, ALU.mult, ALU.min, accum_out=shifts[0][:]
+        )
+        nc.vector.tensor_scalar(
+            negated[:, halves[1]], scores[1][:], -1.0, shifts[0][:], ALU.mult, ALU.min, accum_out=shifts[1][:]
+        )
         weights = sb.tile([P, I], F32, name="weights")
         total = sb.tile([P, 1], F32, name="total")
-        nc.scalar.activation(weights[:], scores[:], ACT.Exp, bias=shift[:], accum_out=total[:])
+        nc.scalar.activation(weights[:], negated[:], ACT.Exp, bias=shifts[1][:], scale=-1.0, accum_out=total[:])
         inverse = sb.tile([P, 1], F32, name="inverse")
         nc.vector.reciprocal(inverse[:], total[:])
-        result = sb.tile([P, I], F32, name="result")
-        nc.vector.tensor_scalar(result[:], weights[:], inverse[:], float(I), ALU.mult, ALU.mult)
-        nc.sync.dma_start(out, result[:])
+        for h, (cols, queue) in enumerate(zip(halves, (nc.sync, nc.scalar))):
+            result = sb.tile([P, HALF], F32, name=f"result{h}")
+            nc.vector.tensor_scalar(result[:], weights[:, cols], inverse[:], float(I), ALU.mult, ALU.mult)
+            queue.dma_start(out[:, cols], result[:])

@@ -219,7 +219,6 @@ def tile_attend_mla_expand_kernel(tc, lat_words, lat_scales, wuk, query, krot, c
         nc.scalar.activation(weights[:], negated[:], ACT.Exp, bias=shifts[1][:], scale=-1.0, accum_out=total[:])
         inverse = sb.tile([P, 1], F32, name="inverse")
         nc.vector.reciprocal(inverse[:], total[:])
-        for h, (cols, queue) in enumerate(zip(halves, (nc.sync, nc.scalar))):
-            result = sb.tile([P, HALF], F32, name=f"result{h}")
-            nc.vector.tensor_scalar(result[:], weights[:, cols], inverse[:], float(I), ALU.mult, ALU.mult)
-            queue.dma_start(out[:, cols], result[:])
+        result = sb.tile([P, I], F32, name="result")
+        nc.vector.tensor_scalar(result[:], weights[:], inverse[:], float(I), ALU.mult, ALU.mult)
+        nc.sync.dma_start(out, result[:])

@@ -37,112 +37,121 @@ def tile_attend_mla_expand_kernel(tc, lat_words, lat_scales, wuk, query, krot, c
         k_pool = [sb.tile([P, T], F32, name=f"k_pool{t}") for t in range(PACK)]
         c_pool = [sb.tile([P, U], F32, name=f"c_pool{u}") for u in range(2)]
         s_pool = [sb.tile([P, U], F32, name=f"s_pool{u}") for u in range(2)]
-        word_pool = sb.tile([P, T], I32, name="word_pool")
+        word_pool = sb.tile([P, T], I32, name="word_pool", align_bytes=64)
         byte_pool = sb.tile([P, T], U8, name="byte_pool")
-        w_raw = sb.tile([P, PACK, D], F32, name="w_raw")
-        q_raw = sb.tile([P, PACK, Q], F32, name="q_raw")
-        qr_raw = sb.tile([P, PACK, Q], F32, name="qr_raw")
+        w_raw = [sb.tile([P, PACK, D // 2], F32, name=f"w_raw{h}") for h in range(2)]
 
-        warm_in = sb.tile([P, 1], F32, name="warm_in")
-        warm_out = sb.tile([P, 1], F32, name="warm_out")
+        queries_raw = [sb.tile([P, PACK, Q], F32, name=f"queries_raw{n}", align_bytes=64) for n in range(2)]
+        lat_bytes = sb.tile([P, I], U8, name="lat_bytes", align_bytes=64)
+        picked_bytes = sb.tile([P, I], U8, name="picked_bytes")
         nc.vector.memset(byte_pool[:].bitcast(I32), 0)
-        nc.vector.memset(warm_in[:], 0.0)
-        nc.scalar.activation(warm_out[:], warm_in[:], ACT.Exp)
+        nc.vector.memset(lat_bytes[:].bitcast(I32), 0)
 
-        nc.sync.dma_start(w_raw[:], wuk.rearrange("(p j) d -> p j d", j=PACK))
-        for g in range(2):
-            nc.sync.dma_start(
-                byte_pool[64 * g : 64 * g + 32 : 4, :].bitcast(I32),
-                lat_scales[0, 8 * g : 8 * g + 8, :].bitcast(I32),
-            )
-        nc.sync.dma_start(tokens[:], offs)
         nc.sync.dma_start(c_pool[0][:], c_rows[:, 0, :])
         nc.sync.dma_start(places[:], offs2)
-        nc.sync.dma_start(s_pool[0][:], s_rows[:, 0, :])
+        nc.sync.dma_start(tokens[:], offs)
+        nc.sync.dma_start(byte_pool[0:P:8, :].bitcast(I32), lat_scales[0].bitcast(I32))
         nc.sync.dma_start(k_pool[0][:], k_rows[:, 0, :])
-        picked_bytes = sb.tile([P, I], U8, name="picked_bytes")
-        nc.vector.tensor_copy(picked_bytes[:], byte_pool[:].indirect(tokens[:]))
-        lat_bytes = sb.tile([P, I], U8, name="lat_bytes", align_bytes=64)
-        nc.vector.memset(lat_bytes[:].bitcast(I32), 0)
-        for g in range(4):
-            first = 64 * (g // 2) + 16 * (g % 2)
-            nc.sync.dma_start(
-                lat_bytes[32 * g : 32 * g + 4, :].bitcast(I32),
-                picked_bytes[first : first + 16 : 4, :].bitcast(I32),
-            )
-
+        nc.sync.dma_start(s_pool[0][:], s_rows[:, 0, :])
         nc.sync.dma_start(k_pool[1][:], k_rows[:, 1, :])
-        nc.sync.dma_start(word_pool[:], lat_words[0].rearrange("p n t -> p (n t)").bitcast(I32))
         nc.sync.dma_start(c_pool[1][:], c_rows[:, 2, :])
+        nc.vector.tensor_copy(picked_bytes[:], byte_pool[:].indirect(tokens[:]))
         nc.sync.dma_start(s_pool[1][:], s_rows[:, 2, :])
+        for j in range(4):
+            nc.sync.dma_start(lat_bytes[j:P:32, :].bitcast(I32), picked_bytes[8 * j : P : 32, :].bitcast(I32))
         nc.sync.dma_start(k_pool[2][:], k_rows[:, 2, :])
         nc.sync.dma_start(k_pool[3][:], k_rows[:, 3, :])
-        nc.sync.dma_start(q_raw[:], query.rearrange("(p j) q -> p j q", j=PACK))
-        nc.sync.dma_start(qr_raw[:], qrot.rearrange("(p j) q -> p j q", j=PACK))
+        for h in range(2):
+            nc.sync.dma_start(w_raw[h][:], wuk.rearrange("(p j) d -> p j d", j=PACK)[:, :, h * D // 2 : (h + 1) * D // 2])
+        nc.sync.dma_start(word_pool[:], lat_words[0].rearrange("p n t -> p (n t)").bitcast(I32))
+        nc.sync.dma_start(queries_raw[0][:], query.rearrange("(p j) q -> p j q", j=PACK))
+        nc.sync.dma_start(queries_raw[1][:], qrot.rearrange("(p j) q -> p j q", j=PACK))
 
-        def quantise(name, grouped, width):
-            codes = sb.tile([P, width], U32, name=f"{name}_codes", align_bytes=64)
+        def quantise(name, grouped, width, tag=None):
+            codes = sb.tile([P, width], U32, name=f"{name}_codes", tag=tag or f"{name}_codes", align_bytes=64)
             scales = sb.tile([P, width], U8, name=f"{name}_scales", align_bytes=64)
             nc.vector.quantize_mx(out=codes[:].bitcast(FP8X4), scales=scales[:], in_=grouped)
             return codes, scales
 
-        def factors(u):
-            trig = sb.tile([P, 3, I], F32, name=f"trig{u}")
-            nc.vector.tensor_copy(trig[:, 1, :], c_pool[u][:].indirect(places[:]))
-            nc.vector.tensor_copy(trig[:, 2, :], s_pool[u][:].indirect(places[:]))
-            nc.scalar.activation(trig[:, 0, :], trig[:, 2, :], ACT.Copy, scale=-1.0)
-            return trig
+        halves = [slice(h * HALF, (h + 1) * HALF) for h in range(2)]
+        chunks = [slice(n * CHUNK, (n + 1) * CHUNK) for n in range(I // CHUNK)]
 
-        def products(t, factor_pair, cols, tag):
-            n = cols.stop - cols.start
-            keys = sb.tile([P, n], F32, name=f"keys{t}{tag}")
-            nc.vector.tensor_copy(keys[:], k_pool[t][:].indirect(tokens[:, cols.start // 16 : cols.stop // 16]))
-            prod = sb.tile([P, 2, n], F32, name=f"prod{t}{tag}")
-            nc.vector.tensor_tensor(
-                prod[:], keys[:].unsqueeze(1).to_broadcast([P, 2, n]), factor_pair[:, :, cols], ALU.mult
-            )
+        def gathered(name, pool, offsets):
+            picked = sb.tile([P, I], F32, name=name)
+            nc.vector.tensor_copy(picked[:], pool[:].indirect(offsets[:]))
+            return picked
+
+        def products_on_gpsimd(name, keys, cos, sin):
+            prod = sb.tile([P, 2, I], F32, name=name)
+            nc.gpsimd.tensor_tensor(prod[:, 0, :], keys[:], cos[:], ALU.mult)
+            nc.gpsimd.tensor_tensor(prod[:, 1, :], keys[:], sin[:], ALU.mult)
             return prod
 
-        def rotate(u, even, odd, cols):
-            nc.vector.tensor_tensor(
-                pairs[:, u, cols, :].rearrange("p (c i) e -> p c e i", i=RUN),
-                even.rearrange("p e (c i) -> p c e i", i=RUN),
-                odd.rearrange("p e (c i) -> p c e i", i=RUN),
-                ALU.add,
-            )
+        cos0 = gathered("cos0", c_pool[0], places)
+        keys0 = gathered("keys0", k_pool[0], tokens)
+        sin0 = gathered("sin0", s_pool[0], places)
+        prod0 = products_on_gpsimd("prod0", keys0, cos0, sin0)
+        keys1 = gathered("keys1", k_pool[1], tokens)
+        prod1 = products_on_gpsimd("prod1", keys1, cos0, sin0)
+        planes = sb.tile([P, 2, I], BF16, name="planes")
+        nc.gpsimd.tensor_tensor(planes[:, 0, :], prod0[:, 0, :], prod1[:, 1, :], ALU.subtract)
+        nc.gpsimd.tensor_tensor(planes[:, 1, :], prod1[:, 0, :], prod0[:, 1, :], ALU.add)
+        pairs = sb.tile([P, 2, I, 2], BF16, name="pairs", align_bytes=64)
+        nc.scalar.copy(
+            pairs[:, 0].rearrange("p (c i) e -> p c e i", i=RUN),
+            planes[:].rearrange("p e (c i) -> p c e i", i=RUN),
+        )
 
-        whole = slice(0, I)
+        cos1 = gathered("cos1", c_pool[1], places)
+        sin1 = gathered("sin1", s_pool[1], places)
+        keys2 = gathered("keys2", k_pool[2], tokens)
+        prod2 = sb.tile([P, 2, I], F32, name="prod2")
+        nc.vector.tensor_tensor(prod2[:, 1, :], keys2[:], sin1[:], ALU.mult)
+        nc.gpsimd.tensor_tensor(prod2[:, 0, :], keys2[:], cos1[:], ALU.mult)
+        keys3 = gathered("keys3", k_pool[3], tokens)
+        prod3 = sb.tile([P, 2, I], F32, name="prod3")
+        nc.vector.scalar_tensor_tensor(prod3[:, 0, :], keys3[:], -1.0, sin1[:], ALU.mult, ALU.mult)
+        nc.vector.tensor_tensor(prod3[:, 1, :], keys3[:], cos1[:], ALU.mult)
+        nc.vector.tensor_tensor(
+            pairs[:, 1].rearrange("p (c i) e -> p c e i", i=RUN),
+            prod2[:].rearrange("p e (c i) -> p c e i", i=RUN),
+            prod3[:].rearrange("p e (c i) -> p c e i", i=RUN),
+            ALU.add,
+        )
+
         w_grouped = sb.tile([P, PACK, P, PACK], BF16, name="w_grouped", align_bytes=64)
-        for u in range(2):
+        for h in range(2):
             nc.scalar.copy(
-                w_grouped[:, 2 * u : 2 * u + 2].rearrange("p t m j -> p m j t"),
-                w_raw[:].rearrange("p j (m t) -> p m j t", t=PACK)[:, :, :, 2 * u : 2 * u + 2],
+                w_grouped[:, :, h * P // 2 : (h + 1) * P // 2, :].rearrange("p t m j -> p m j t"),
+                w_raw[h][:].rearrange("p j (m t) -> p m j t", t=PACK),
             )
         w_codes, w_scales = quantise("w", w_grouped[:].rearrange("p t m j -> p (t m j)"), D)
 
-        cos0 = sb.tile([P, I], F32, name="cos0")
-        sin0 = sb.tile([P, I], F32, name="sin0")
-        nc.vector.tensor_copy(cos0[:], c_pool[0][:].indirect(places[:]))
-        nc.vector.tensor_copy(sin0[:], s_pool[0][:].indirect(places[:]))
-        terms = []
-        for t in range(2):
-            keys = sb.tile([P, I], F32, name=f"keys{t}")
-            nc.vector.tensor_copy(keys[:], k_pool[t][:].indirect(tokens[:]))
-            by_cos = sb.tile([P, I], F32, name=f"by_cos{t}")
-            by_sin = sb.tile([P, I], F32, name=f"by_sin{t}")
-            nc.gpsimd.tensor_tensor(by_cos[:], keys[:], cos0[:], ALU.mult)
-            nc.gpsimd.tensor_tensor(by_sin[:], keys[:], sin0[:], ALU.mult)
-            terms.append((by_cos, by_sin))
-        planes = sb.tile([P, 2, I], BF16, name="planes")
-        nc.gpsimd.tensor_tensor(planes[:, 0, :], terms[0][0][:], terms[1][1][:], ALU.subtract)
-        nc.gpsimd.tensor_tensor(planes[:, 1, :], terms[1][0][:], terms[0][1][:], ALU.add)
+        km_grouped = sb.tile([P, I, PACK], BF16, name="km_grouped", align_bytes=64)
+        pair_words = pairs[:].rearrange("p u i e -> p u (i e)").bitcast(F32)
+        for h, cols in enumerate(halves):
+            nc.scalar.copy(
+                km_grouped[:, cols].rearrange("p i t -> p (i t)").bitcast(F32).rearrange("p (c i u) -> p c u i", i=RUN, u=2),
+                pair_words[:, :, cols].rearrange("p u (c i) -> p c u i", i=RUN),
+            )
 
-        lat_codes = sb.tile([P, I], U32, name="lat_codes", align_bytes=64)
-        nc.vector.tensor_copy(lat_codes[:], word_pool[:].bitcast(U32).indirect(tokens[:]))
+        q_grouped = sb.tile([P, 2, Q, PACK], BF16, name="q_grouped", tag="w_grouped", align_bytes=64)
+        for n in range(2):
+            nc.scalar.copy(
+                q_grouped[:, n].rearrange("p (c i) j -> p c j i", i=RUN),
+                queries_raw[n][:].rearrange("p j (c i) -> p c j i", i=RUN),
+            )
 
-        b_grouped = sb.tile([P, I, PACK], BF16, name="b_grouped", align_bytes=64)
-        for n in range(I // CHUNK):
-            cols = slice(n * CHUNK, (n + 1) * CHUNK)
+        lat_codes = [sb.tile([P, HALF], U32, name=f"lat_codes{h}", align_bytes=64) for h in range(2)]
+        for h, cols in enumerate(halves):
+            nc.vector.tensor_copy(
+                lat_codes[h][:], word_pool[:].bitcast(U32).indirect(tokens[:, cols.start // 16 : cols.stop // 16])
+            )
+        km_codes, km_scales = quantise("km", km_grouped[:].rearrange("p i t -> p (i t)"), I, tag="word_pool")
+        q_codes, q_scales = quantise("q", q_grouped[:].rearrange("p n q j -> p (n q j)"), 2 * Q)
+
+        b_grouped = sb.tile([P, I, PACK], BF16, name="b_grouped", tag="queries_raw1", align_bytes=64)
+        for n, cols in enumerate(chunks):
             bank = ps.tile([P, PACK, CHUNK], F32, name=f"b_bank{n}")
             for t in range(PACK):
                 rows = slice(t * P, (t + 1) * P)
@@ -150,73 +159,48 @@ def tile_attend_mla_expand_kernel(tc, lat_words, lat_scales, wuk, query, krot, c
                     out=bank[:, t, :],
                     lhsT=w_codes[:, rows].bitcast(FP8X4),
                     lhsT_scale=w_scales[:, rows],
-                    rhs=lat_codes[:, cols].bitcast(FP8X4),
+                    rhs=lat_codes[n // 2][:, chunks[n % 2]].bitcast(FP8X4),
                     rhs_scale=lat_bytes[:, cols],
                     start=True,
                     stop=True,
                 )
-            nc.scalar.copy(b_grouped[:, cols, :], bank[:].rearrange("p t i -> p i t"))
+            copy = nc.vector.tensor_copy if n == 2 else nc.scalar.copy
+            copy(b_grouped[:, cols, :], bank[:].rearrange("p t i -> p i t"))
 
-        trig1 = factors(1)
-        pairs = sb.tile([P, 2, I, 2], BF16, name="pairs", tag="lat_codes", align_bytes=64)
-        nc.scalar.copy(
-            pairs[:, 0].rearrange("p (c i) e -> p c e i", i=RUN),
-            planes[:].rearrange("p e (c i) -> p c e i", i=RUN),
-        )
-        b_codes, b_scales = quantise("b", b_grouped[:].rearrange("p i t -> p (i t)"), I)
-        prod2 = products(2, trig1[:, 1:3, :], whole, "")
-
-        halves = [slice(h * HALF, (h + 1) * HALF) for h in range(2)]
-        prod3 = [products(3, trig1[:, 0:2, :], cols, f"h{h}") for h, cols in enumerate(halves)]
-        for h, cols in enumerate(halves):
-            rotate(1, prod2[:, :, cols], prod3[h][:], cols)
-        km_grouped = [sb.tile([P, HALF, PACK], BF16, name=f"km_grouped{h}", align_bytes=64) for h in range(2)]
-        pair_words = pairs[:].rearrange("p u i e -> p u (i e)").bitcast(F32)
-        for h, cols in enumerate(halves):
-            nc.scalar.copy(
-                km_grouped[h][:].rearrange("p i t -> p (i t)").bitcast(F32).rearrange("p (c i u) -> p c u i", i=RUN, u=2),
-                pair_words[:, :, cols].rearrange("p u (c i) -> p c u i", i=RUN),
-            )
-        q_grouped = sb.tile([P, 2, Q, PACK], BF16, name="q_grouped", align_bytes=64)
-        for n, raw in enumerate((q_raw, qr_raw)):
-            nc.scalar.copy(
-                q_grouped[:, n].rearrange("p (c i) j -> p c j i", i=RUN),
-                raw[:].rearrange("p j (c i) -> p c j i", i=RUN),
-            )
-        q_codes, q_scales = quantise("q", q_grouped[:].rearrange("p n q j -> p (n q j)"), 2 * Q)
-
-        scores = [ps.tile([P, HALF], F32, name=f"scores{h}") for h in range(2)]
-        for h, cols in enumerate(halves):
-            km_codes, km_scales = quantise(f"km{h}", km_grouped[h][:].rearrange("p i t -> p (i t)"), HALF)
+        negated = sb.tile([P, I], F32, name="negated", tag="queries_raw1", align_bytes=64)
+        parts = [halves[0], chunks[2], chunks[3]]
+        banks = []
+        for n, cols in enumerate(parts):
+            width = cols.stop - cols.start
+            b_codes, b_scales = quantise(f"b{n}", b_grouped[:, cols, :].rearrange("p i t -> p (i t)"), width)
+            scores = ps.tile([P, width], F32, name=f"scores{n}", tag=f"b_bank{(n + 1) % 3}")
             nc.tensor.matmul_mx(
-                out=scores[h][:],
-                lhsT=q_codes[:, :Q].bitcast(FP8X4),
-                lhsT_scale=q_scales[:, :Q],
-                rhs=b_codes[:, cols].bitcast(FP8X4),
-                rhs_scale=b_scales[:, cols],
+                out=scores[:],
+                lhsT=q_codes[:, Q:].bitcast(FP8X4),
+                lhsT_scale=q_scales[:, Q:],
+                rhs=km_codes[:, cols].bitcast(FP8X4),
+                rhs_scale=km_scales[:, cols],
                 start=True,
                 stop=False,
             )
             nc.tensor.matmul_mx(
-                out=scores[h][:],
-                lhsT=q_codes[:, Q:].bitcast(FP8X4),
-                lhsT_scale=q_scales[:, Q:],
-                rhs=km_codes[:].bitcast(FP8X4),
-                rhs_scale=km_scales[:],
+                out=scores[:],
+                lhsT=q_codes[:, :Q].bitcast(FP8X4),
+                lhsT_scale=q_scales[:, :Q],
+                rhs=b_codes[:].bitcast(FP8X4),
+                rhs_scale=b_scales[:],
                 start=False,
                 stop=True,
             )
-        negated = sb.tile([P, I], F32, name="negated")
-        shifts = [sb.tile([P, 1], F32, name=f"shift{h}") for h in range(2)]
-        nc.vector.tensor_scalar(
-            negated[:, halves[0]], scores[0][:], -1.0, None, ALU.mult, ALU.min, accum_out=shifts[0][:]
-        )
-        nc.vector.tensor_scalar(
-            negated[:, halves[1]], scores[1][:], -1.0, shifts[0][:], ALU.mult, ALU.min, accum_out=shifts[1][:]
-        )
+            banks.append(scores)
+        start_value = None
+        for n, cols in enumerate(parts):
+            shift = sb.tile([P, 1], F32, name=f"shift{n}")
+            nc.vector.tensor_scalar(negated[:, cols], banks[n][:], -1.0, start_value, ALU.mult, ALU.min, accum_out=shift[:])
+            start_value = shift[:]
         weights = sb.tile([P, I], F32, name="weights")
         total = sb.tile([P, 1], F32, name="total")
-        nc.scalar.activation(weights[:], negated[:], ACT.Exp, bias=shifts[1][:], scale=-1.0, accum_out=total[:])
+        nc.scalar.activation(weights[:], negated[:], ACT.Exp, bias=shift[:], scale=-1.0, accum_out=total[:])
         inverse = sb.tile([P, 1], F32, name="inverse")
         nc.vector.reciprocal(inverse[:], total[:])
         result = sb.tile([P, I], F32, name="result")

@@ -36,10 +36,10 @@ def tile_attend_mla_expand_kernel(tc, lat_words, lat_scales, wuk, query, krot, c
         s_rows = sinn.rearrange("(p t) n -> p t n", t=PACK)
         k_pool = [sb.tile([P, T], F32, name=f"k_pool{t}") for t in range(PACK)]
         c_pool = [sb.tile([P, U], F32, name=f"c_pool{u}") for u in range(2)]
-        s_pool = [sb.tile([P, U], F32, name=f"s_pool{u}") for u in range(2)]
+        s_pool = [sb.tile([P, U], F32, name=f"s_pool{u}", align_bytes=64) for u in range(2)]
         word_pool = sb.tile([P, T], I32, name="word_pool", align_bytes=64)
         byte_pool = sb.tile([P, T], U8, name="byte_pool")
-        w_raw = [sb.tile([P, PACK, D // 2], F32, name=f"w_raw{h}") for h in range(2)]
+        w_raw = [sb.tile([P, PACK, D // 2], F32, name=f"w_raw{h}", align_bytes=64) for h in range(2)]
 
         queries_raw = [sb.tile([P, PACK, Q], F32, name=f"queries_raw{n}", align_bytes=64) for n in range(2)]
         lat_bytes = sb.tile([P, I], U8, name="lat_bytes", align_bytes=64)
@@ -96,28 +96,35 @@ def tile_attend_mla_expand_kernel(tc, lat_words, lat_scales, wuk, query, krot, c
         planes = sb.tile([P, 2, I], BF16, name="planes")
         nc.gpsimd.tensor_tensor(planes[:, 0, :], prod0[:, 0, :], prod1[:, 1, :], ALU.subtract)
         nc.gpsimd.tensor_tensor(planes[:, 1, :], prod1[:, 0, :], prod0[:, 1, :], ALU.add)
-        pairs = sb.tile([P, 2, I, 2], BF16, name="pairs", align_bytes=64)
+
+        trig = sb.tile([P, 3, I], F32, name="trig")
+        nc.vector.tensor_copy(trig[:, 1, :], c_pool[1][:].indirect(places[:]))
+        nc.vector.tensor_copy(trig[:, 2, :], s_pool[1][:].indirect(places[:]))
+        nc.scalar.activation(trig[:, 0, :], trig[:, 2, :], ACT.Copy, scale=-1.0)
+        pairs = sb.tile([P, 2, I, 2], BF16, name="pairs", tag="s_pool1", align_bytes=64)
         nc.scalar.copy(
             pairs[:, 0].rearrange("p (c i) e -> p c e i", i=RUN),
             planes[:].rearrange("p e (c i) -> p c e i", i=RUN),
         )
-
-        cos1 = gathered("cos1", c_pool[1], places)
-        sin1 = gathered("sin1", s_pool[1], places)
         keys2 = gathered("keys2", k_pool[2], tokens)
         prod2 = sb.tile([P, 2, I], F32, name="prod2")
-        nc.vector.tensor_tensor(prod2[:, 1, :], keys2[:], sin1[:], ALU.mult)
-        nc.gpsimd.tensor_tensor(prod2[:, 0, :], keys2[:], cos1[:], ALU.mult)
-        keys3 = gathered("keys3", k_pool[3], tokens)
-        prod3 = sb.tile([P, 2, I], F32, name="prod3")
-        nc.vector.scalar_tensor_tensor(prod3[:, 0, :], keys3[:], -1.0, sin1[:], ALU.mult, ALU.mult)
-        nc.vector.tensor_tensor(prod3[:, 1, :], keys3[:], cos1[:], ALU.mult)
-        nc.vector.tensor_tensor(
-            pairs[:, 1].rearrange("p (c i) e -> p c e i", i=RUN),
-            prod2[:].rearrange("p e (c i) -> p c e i", i=RUN),
-            prod3[:].rearrange("p e (c i) -> p c e i", i=RUN),
-            ALU.add,
-        )
+        nc.vector.tensor_tensor(prod2[:, 1, :], keys2[:], trig[:, 2, :], ALU.mult)
+        nc.gpsimd.tensor_tensor(prod2[:, 0, :], keys2[:], trig[:, 1, :], ALU.mult)
+        keys3 = [sb.tile([P, HALF], F32, name=f"keys3_{h}") for h in range(2)]
+        prod3 = [sb.tile([P, 2, HALF], F32, name=f"prod3_{h}") for h in range(2)]
+        for h, cols in enumerate(halves):
+            nc.vector.tensor_copy(keys3[h][:], k_pool[3][:].indirect(tokens[:, cols.start // 16 : cols.stop // 16]))
+        for h, cols in enumerate(halves):
+            nc.vector.tensor_tensor(
+                prod3[h][:], keys3[h][:].unsqueeze(1).to_broadcast([P, 2, HALF]), trig[:, 0:2, cols], ALU.mult
+            )
+        for h, cols in enumerate(halves):
+            nc.vector.tensor_tensor(
+                pairs[:, 1, cols].rearrange("p (c i) e -> p c e i", i=RUN),
+                prod2[:, :, cols].rearrange("p e (c i) -> p c e i", i=RUN),
+                prod3[h][:].rearrange("p e (c i) -> p c e i", i=RUN),
+                ALU.add,
+            )
 
         w_grouped = sb.tile([P, PACK, P, PACK], BF16, name="w_grouped", align_bytes=64)
         for h in range(2):
@@ -127,7 +134,7 @@ def tile_attend_mla_expand_kernel(tc, lat_words, lat_scales, wuk, query, krot, c
             )
         w_codes, w_scales = quantise("w", w_grouped[:].rearrange("p t m j -> p (t m j)"), D)
 
-        km_grouped = sb.tile([P, I, PACK], BF16, name="km_grouped", align_bytes=64)
+        km_grouped = sb.tile([P, I, PACK], BF16, name="km_grouped", tag="w_raw1", align_bytes=64)
         pair_words = pairs[:].rearrange("p u i e -> p u (i e)").bitcast(F32)
         for h, cols in enumerate(halves):
             nc.scalar.copy(
@@ -150,7 +157,7 @@ def tile_attend_mla_expand_kernel(tc, lat_words, lat_scales, wuk, query, krot, c
         km_codes, km_scales = quantise("km", km_grouped[:].rearrange("p i t -> p (i t)"), I, tag="word_pool")
         q_codes, q_scales = quantise("q", q_grouped[:].rearrange("p n q j -> p (n q j)"), 2 * Q)
 
-        b_grouped = sb.tile([P, I, PACK], BF16, name="b_grouped", tag="queries_raw1", align_bytes=64)
+        b_grouped = sb.tile([P, I * PACK], BF16, name="b_grouped", tag="queries_raw1", align_bytes=64)
         for n, cols in enumerate(chunks):
             bank = ps.tile([P, PACK, CHUNK], F32, name=f"b_bank{n}")
             for t in range(PACK):
@@ -165,17 +172,21 @@ def tile_attend_mla_expand_kernel(tc, lat_words, lat_scales, wuk, query, krot, c
                     stop=True,
                 )
             copy = nc.vector.tensor_copy if n == 2 else nc.scalar.copy
-            copy(b_grouped[:, cols, :], bank[:].rearrange("p t i -> p i t"))
+            copy(b_grouped[:, PACK * cols.start : PACK * cols.stop].rearrange("p (i t) -> p i t", t=PACK), bank[:].rearrange("p t i -> p i t"))
 
-        negated = sb.tile([P, I], F32, name="negated", tag="queries_raw1", align_bytes=64)
-        parts = [halves[0], chunks[2], chunks[3]]
-        banks = []
+        negated = sb.tile([P, I], F32, name="negated")
+        parts = chunks
+        spans = [slice(0, I - CHUNK), chunks[-1]]
+        banks = [
+            ps.tile([P, span.stop - span.start], F32, name=f"scores{h}", tag=f"b_bank{h + 1}")
+            for h, span in enumerate(spans)
+        ]
         for n, cols in enumerate(parts):
             width = cols.stop - cols.start
-            b_codes, b_scales = quantise(f"b{n}", b_grouped[:, cols, :].rearrange("p i t -> p (i t)"), width)
-            scores = ps.tile([P, width], F32, name=f"scores{n}", tag=f"b_bank{(n + 1) % 3}")
+            b_codes, b_scales = quantise(f"b{n}", b_grouped[:, PACK * cols.start : PACK * cols.stop], width)
+            scores = banks[1][:] if cols == spans[1] else banks[0][:, cols]
             nc.tensor.matmul_mx(
-                out=scores[:],
+                out=scores,
                 lhsT=q_codes[:, Q:].bitcast(FP8X4),
                 lhsT_scale=q_scales[:, Q:],
                 rhs=km_codes[:, cols].bitcast(FP8X4),
@@ -184,7 +195,7 @@ def tile_attend_mla_expand_kernel(tc, lat_words, lat_scales, wuk, query, krot, c
                 stop=False,
             )
             nc.tensor.matmul_mx(
-                out=scores[:],
+                out=scores,
                 lhsT=q_codes[:, :Q].bitcast(FP8X4),
                 lhsT_scale=q_scales[:, :Q],
                 rhs=b_codes[:].bitcast(FP8X4),
@@ -192,9 +203,8 @@ def tile_attend_mla_expand_kernel(tc, lat_words, lat_scales, wuk, query, krot, c
                 start=False,
                 stop=True,
             )
-            banks.append(scores)
         start_value = None
-        for n, cols in enumerate(parts):
+        for n, cols in enumerate(spans):
             shift = sb.tile([P, 1], F32, name=f"shift{n}")
             nc.vector.tensor_scalar(negated[:, cols], banks[n][:], -1.0, start_value, ALU.mult, ALU.min, accum_out=shift[:])
             start_value = shift[:]

@@ -172,7 +172,10 @@ def tile_attend_mla_expand_kernel(tc, lat_words, lat_scales, wuk, query, krot, c
                     stop=True,
                 )
             copy = nc.vector.tensor_copy if n == 2 else nc.scalar.copy
-            copy(b_grouped[:, PACK * cols.start : PACK * cols.stop].rearrange("p (i t) -> p i t", t=PACK), bank[:].rearrange("p t i -> p i t"))
+            copy(
+                b_grouped[:, PACK * cols.start : PACK * cols.stop].rearrange("p (c i t) -> p c t i", i=2, t=PACK),
+                bank[:].rearrange("p t (c i) -> p c t i", i=2),
+            )
 
         negated = sb.tile([P, I], F32, name="negated")
         parts = chunks

@@ -36,12 +36,12 @@ def tile_attend_mla_expand_kernel(tc, lat_words, lat_scales, wuk, query, krot, c
         s_rows = sinn.rearrange("(p t) n -> p t n", t=PACK)
         k_pool = [sb.tile([P, T], F32, name=f"k_pool{t}") for t in range(PACK)]
         c_pool = [sb.tile([P, U], F32, name=f"c_pool{u}") for u in range(2)]
-        s_pool = [sb.tile([P, U], F32, name=f"s_pool{u}", align_bytes=64) for u in range(2)]
+        s_pool = [sb.tile([P, U], F32, name=f"s_pool{u}") for u in range(2)]
         word_pool = sb.tile([P, T], I32, name="word_pool", align_bytes=64)
         byte_pool = sb.tile([P, T], U8, name="byte_pool")
         w_raw = [sb.tile([P, PACK, D // 2], F32, name=f"w_raw{h}", align_bytes=64) for h in range(2)]
-
-        queries_raw = [sb.tile([P, PACK, Q], F32, name=f"queries_raw{n}", align_bytes=64) for n in range(2)]
+        query_raw = sb.tile([P, PACK, Q], F32, name="query_raw", align_bytes=64)
+        qrot_raw = sb.tile([P, PACK, Q], F32, name="qrot_raw", align_bytes=64)
         lat_bytes = sb.tile([P, I], U8, name="lat_bytes", align_bytes=64)
         picked_bytes = sb.tile([P, I], U8, name="picked_bytes")
         nc.vector.memset(byte_pool[:].bitcast(I32), 0)
@@ -51,8 +51,8 @@ def tile_attend_mla_expand_kernel(tc, lat_words, lat_scales, wuk, query, krot, c
         nc.sync.dma_start(places[:], offs2)
         nc.sync.dma_start(tokens[:], offs)
         nc.sync.dma_start(byte_pool[0:P:8, :].bitcast(I32), lat_scales[0].bitcast(I32))
-        nc.sync.dma_start(k_pool[0][:], k_rows[:, 0, :])
         nc.sync.dma_start(s_pool[0][:], s_rows[:, 0, :])
+        nc.sync.dma_start(k_pool[0][:], k_rows[:, 0, :])
         nc.sync.dma_start(k_pool[1][:], k_rows[:, 1, :])
         nc.sync.dma_start(c_pool[1][:], c_rows[:, 2, :])
         nc.vector.tensor_copy(picked_bytes[:], byte_pool[:].indirect(tokens[:]))
@@ -64,8 +64,8 @@ def tile_attend_mla_expand_kernel(tc, lat_words, lat_scales, wuk, query, krot, c
         for h in range(2):
             nc.sync.dma_start(w_raw[h][:], wuk.rearrange("(p j) d -> p j d", j=PACK)[:, :, h * D // 2 : (h + 1) * D // 2])
         nc.sync.dma_start(word_pool[:], lat_words[0].rearrange("p n t -> p (n t)").bitcast(I32))
-        nc.sync.dma_start(queries_raw[0][:], query.rearrange("(p j) q -> p j q", j=PACK))
-        nc.sync.dma_start(queries_raw[1][:], qrot.rearrange("(p j) q -> p j q", j=PACK))
+        nc.sync.dma_start(query_raw[:], query.rearrange("(p j) q -> p j q", j=PACK))
+        nc.sync.dma_start(qrot_raw[:], qrot.rearrange("(p j) q -> p j q", j=PACK))
 
         def quantise(name, grouped, width, tag=None):
             codes = sb.tile([P, width], U32, name=f"{name}_codes", tag=tag or f"{name}_codes", align_bytes=64)
@@ -76,55 +76,47 @@ def tile_attend_mla_expand_kernel(tc, lat_words, lat_scales, wuk, query, krot, c
         halves = [slice(h * HALF, (h + 1) * HALF) for h in range(2)]
         chunks = [slice(n * CHUNK, (n + 1) * CHUNK) for n in range(I // CHUNK)]
 
-        def gathered(name, pool, offsets):
-            picked = sb.tile([P, I], F32, name=name)
-            nc.vector.tensor_copy(picked[:], pool[:].indirect(offsets[:]))
-            return picked
+        def listed(offsets, cols):
+            return offsets[:, cols.start // 16 : cols.stop // 16]
 
-        def products_on_gpsimd(name, keys, cos, sin):
-            prod = sb.tile([P, 2, I], F32, name=name)
-            nc.gpsimd.tensor_tensor(prod[:, 0, :], keys[:], cos[:], ALU.mult)
-            nc.gpsimd.tensor_tensor(prod[:, 1, :], keys[:], sin[:], ALU.mult)
-            return prod
+        def gather_on_scalar(picked, pool, offsets):
+            nc.scalar.activation(picked, pool[:].indirect(offsets), ACT.Copy)
 
-        cos0 = gathered("cos0", c_pool[0], places)
-        keys0 = gathered("keys0", k_pool[0], tokens)
-        sin0 = gathered("sin0", s_pool[0], places)
-        prod0 = products_on_gpsimd("prod0", keys0, cos0, sin0)
-        keys1 = gathered("keys1", k_pool[1], tokens)
-        prod1 = products_on_gpsimd("prod1", keys1, cos0, sin0)
-        planes = sb.tile([P, 2, I], BF16, name="planes")
-        nc.gpsimd.tensor_tensor(planes[:, 0, :], prod0[:, 0, :], prod1[:, 1, :], ALU.subtract)
-        nc.gpsimd.tensor_tensor(planes[:, 1, :], prod1[:, 0, :], prod0[:, 1, :], ALU.add)
+        def in_runs(view):
+            return view.rearrange("p e (c i) -> p c e i", i=RUN)
 
-        trig = sb.tile([P, 3, I], F32, name="trig")
-        nc.vector.tensor_copy(trig[:, 1, :], c_pool[1][:].indirect(places[:]))
-        nc.vector.tensor_copy(trig[:, 2, :], s_pool[1][:].indirect(places[:]))
-        nc.scalar.activation(trig[:, 0, :], trig[:, 2, :], ACT.Copy, scale=-1.0)
-        pairs = sb.tile([P, 2, I, 2], BF16, name="pairs", tag="s_pool1", align_bytes=64)
-        nc.scalar.copy(
-            pairs[:, 0].rearrange("p (c i) e -> p c e i", i=RUN),
-            planes[:].rearrange("p e (c i) -> p c e i", i=RUN),
-        )
-        keys2 = gathered("keys2", k_pool[2], tokens)
-        prod2 = sb.tile([P, 2, I], F32, name="prod2")
-        nc.vector.tensor_tensor(prod2[:, 1, :], keys2[:], trig[:, 2, :], ALU.mult)
-        nc.gpsimd.tensor_tensor(prod2[:, 0, :], keys2[:], trig[:, 1, :], ALU.mult)
-        keys3 = [sb.tile([P, HALF], F32, name=f"keys3_{h}") for h in range(2)]
-        prod3 = [sb.tile([P, 2, HALF], F32, name=f"prod3_{h}") for h in range(2)]
-        for h, cols in enumerate(halves):
-            nc.vector.tensor_copy(keys3[h][:], k_pool[3][:].indirect(tokens[:, cols.start // 16 : cols.stop // 16]))
-        for h, cols in enumerate(halves):
-            nc.vector.tensor_tensor(
-                prod3[h][:], keys3[h][:].unsqueeze(1).to_broadcast([P, 2, HALF]), trig[:, 0:2, cols], ALU.mult
-            )
-        for h, cols in enumerate(halves):
-            nc.vector.tensor_tensor(
-                pairs[:, 1, cols].rearrange("p (c i) e -> p c e i", i=RUN),
-                prod2[:, :, cols].rearrange("p e (c i) -> p c e i", i=RUN),
-                prod3[h][:].rearrange("p e (c i) -> p c e i", i=RUN),
-                ALU.add,
-            )
+        def gather_on_vector(picked, pool, offsets):
+            nc.vector.tensor_copy(picked, pool[:].indirect(offsets))
+
+        pairs = [sb.tile([P, 2, HALF, 2], BF16, name=f"pairs{h}", align_bytes=64) for h in range(2)]
+        for u in range(2):
+            gather_trig = gather_on_vector if u == 0 else gather_on_scalar
+            trig = sb.tile([P, 3, I], F32, name=f"trig{u}")
+            gather_trig(trig[:, 1, :], c_pool[u], places[:])
+            gather_trig(trig[:, 2, :], s_pool[u], places[:])
+            nc.scalar.activation(trig[:, 0, :], trig[:, 2, :], ACT.Copy, scale=-1.0)
+            first = sb.tile([P, I], F32, name=f"first{u}")
+            second = [sb.tile([P, HALF], F32, name=f"second{u}_{h}") for h in range(2)]
+            for h, cols in enumerate(halves):
+                gather = gather_on_vector if (u, h) == (1, 0) else gather_on_scalar
+                gather(first[:, cols], k_pool[2 * u], listed(tokens, cols))
+            prod_first = sb.tile([P, 2, I], F32, name=f"prod_first{u}")
+            nc.vector.tensor_tensor(prod_first[:], first[:].unsqueeze(1).to_broadcast([P, 2, I]), trig[:, 1:3, :], ALU.mult)
+            prod_second = [sb.tile([P, 2, HALF], F32, name=f"prod_second{u}_{h}") for h in range(2)]
+            for h, cols in enumerate(halves):
+                gather = gather_on_vector if (u, h) == (1, 1) else gather_on_scalar
+                gather(second[h][:], k_pool[2 * u + 1], listed(tokens, cols))
+            for h, cols in enumerate(halves):
+                nc.vector.tensor_tensor(
+                    prod_second[h][:], second[h][:].unsqueeze(1).to_broadcast([P, 2, HALF]), trig[:, 0:2, cols], ALU.mult
+                )
+            for h, cols in enumerate(halves):
+                nc.vector.tensor_tensor(
+                    pairs[h][:, u].rearrange("p (c i) e -> p c e i", i=RUN),
+                    in_runs(prod_first[:, :, cols]),
+                    in_runs(prod_second[h][:]),
+                    ALU.add,
+                )
 
         w_grouped = sb.tile([P, PACK, P, PACK], BF16, name="w_grouped", align_bytes=64)
         for h in range(2):
@@ -134,30 +126,27 @@ def tile_attend_mla_expand_kernel(tc, lat_words, lat_scales, wuk, query, krot, c
             )
         w_codes, w_scales = quantise("w", w_grouped[:].rearrange("p t m j -> p (t m j)"), D)
 
-        km_grouped = sb.tile([P, I, PACK], BF16, name="km_grouped", tag="w_raw1", align_bytes=64)
-        pair_words = pairs[:].rearrange("p u i e -> p u (i e)").bitcast(F32)
+        km_grouped = sb.tile([P, I * PACK], BF16, name="km_grouped", tag="w_raw1", align_bytes=64)
         for h, cols in enumerate(halves):
             nc.scalar.copy(
-                km_grouped[:, cols].rearrange("p i t -> p (i t)").bitcast(F32).rearrange("p (c i u) -> p c u i", i=RUN, u=2),
-                pair_words[:, :, cols].rearrange("p u (c i) -> p c u i", i=RUN),
+                km_grouped[:, PACK * cols.start : PACK * cols.stop].bitcast(F32).rearrange("p (c i u) -> p c u i", i=RUN, u=2),
+                pairs[h][:].rearrange("p u i e -> p u (i e)").bitcast(F32).rearrange("p u (c i) -> p c u i", i=RUN),
             )
 
-        q_grouped = sb.tile([P, 2, Q, PACK], BF16, name="q_grouped", tag="w_grouped", align_bytes=64)
-        for n in range(2):
+        q_grouped = sb.tile([P, 2, Q, PACK], BF16, name="q_grouped", align_bytes=64)
+        for n, raw in enumerate((query_raw, qrot_raw)):
             nc.scalar.copy(
                 q_grouped[:, n].rearrange("p (c i) j -> p c j i", i=RUN),
-                queries_raw[n][:].rearrange("p j (c i) -> p c j i", i=RUN),
+                raw[:].rearrange("p j (c i) -> p c j i", i=RUN),
             )
 
-        lat_codes = [sb.tile([P, HALF], U32, name=f"lat_codes{h}", align_bytes=64) for h in range(2)]
-        for h, cols in enumerate(halves):
-            nc.vector.tensor_copy(
-                lat_codes[h][:], word_pool[:].bitcast(U32).indirect(tokens[:, cols.start // 16 : cols.stop // 16])
-            )
-        km_codes, km_scales = quantise("km", km_grouped[:].rearrange("p i t -> p (i t)"), I, tag="word_pool")
+        lat_codes = [sb.tile([P, CHUNK], U32, name=f"lat_codes{n}", align_bytes=64) for n in range(len(chunks))]
+        for n, cols in enumerate(chunks):
+            nc.vector.tensor_copy(lat_codes[n][:], word_pool[:].bitcast(U32).indirect(listed(tokens, cols)))
+        km_codes, km_scales = quantise("km", km_grouped[:], I, tag="query_raw")
         q_codes, q_scales = quantise("q", q_grouped[:].rearrange("p n q j -> p (n q j)"), 2 * Q)
 
-        b_grouped = sb.tile([P, I * PACK], BF16, name="b_grouped", tag="queries_raw1", align_bytes=64)
+        b_grouped = sb.tile([P, I * PACK], BF16, name="b_grouped", tag="qrot_raw", align_bytes=64)
         for n, cols in enumerate(chunks):
             bank = ps.tile([P, PACK, CHUNK], F32, name=f"b_bank{n}")
             for t in range(PACK):
@@ -166,7 +155,7 @@ def tile_attend_mla_expand_kernel(tc, lat_words, lat_scales, wuk, query, krot, c
                     out=bank[:, t, :],
                     lhsT=w_codes[:, rows].bitcast(FP8X4),
                     lhsT_scale=w_scales[:, rows],
-                    rhs=lat_codes[n // 2][:, chunks[n % 2]].bitcast(FP8X4),
+                    rhs=lat_codes[n][:].bitcast(FP8X4),
                     rhs_scale=lat_bytes[:, cols],
                     start=True,
                     stop=True,
@@ -177,17 +166,11 @@ def tile_attend_mla_expand_kernel(tc, lat_words, lat_scales, wuk, query, krot, c
                 bank[:].rearrange("p t (c i) -> p c t i", i=2),
             )
 
-        negated = sb.tile([P, I], F32, name="negated")
-        parts = chunks
-        spans = [slice(0, I - CHUNK), chunks[-1]]
-        banks = [
-            ps.tile([P, span.stop - span.start], F32, name=f"scores{h}", tag=f"b_bank{h + 1}")
-            for h, span in enumerate(spans)
-        ]
-        for n, cols in enumerate(parts):
-            width = cols.stop - cols.start
-            b_codes, b_scales = quantise(f"b{n}", b_grouped[:, PACK * cols.start : PACK * cols.stop], width)
-            scores = banks[1][:] if cols == spans[1] else banks[0][:, cols]
+        early = ps.tile([P, I - CHUNK], F32, name="scores_early", tag="b_bank1")
+        last = ps.tile([P, CHUNK], F32, name="scores_last", tag="b_bank2")
+        for n, cols in enumerate(chunks):
+            b_codes, b_scales = quantise(f"b{n}", b_grouped[:, PACK * cols.start : PACK * cols.stop], CHUNK)
+            scores = last[:] if n == 3 else early[:, cols]
             nc.tensor.matmul_mx(
                 out=scores,
                 lhsT=q_codes[:, Q:].bitcast(FP8X4),
@@ -206,10 +189,11 @@ def tile_attend_mla_expand_kernel(tc, lat_words, lat_scales, wuk, query, krot, c
                 start=False,
                 stop=True,
             )
+        negated = sb.tile([P, I], F32, name="negated")
         start_value = None
-        for n, cols in enumerate(spans):
+        for n, (scores, cols) in enumerate(((early, slice(0, I - CHUNK)), (last, chunks[3]))):
             shift = sb.tile([P, 1], F32, name=f"shift{n}")
-            nc.vector.tensor_scalar(negated[:, cols], banks[n][:], -1.0, start_value, ALU.mult, ALU.min, accum_out=shift[:])
+            nc.vector.tensor_scalar(negated[:, cols], scores[:], -1.0, start_value, ALU.mult, ALU.min, accum_out=shift[:])
             start_value = shift[:]
         weights = sb.tile([P, I], F32, name="weights")
         total = sb.tile([P, 1], F32, name="total")

@@ -21,6 +21,7 @@ PACK = 4
 CHUNK = 128
 HALF = I // 2
 RUN = 4
+W_SPLIT = 32
 
 
 def tile_attend_mla_expand_kernel(tc, lat_words, lat_scales, wuk, query, krot, cosn, sinn, qrot, offs, offs2, out):
@@ -39,7 +40,7 @@ def tile_attend_mla_expand_kernel(tc, lat_words, lat_scales, wuk, query, krot, c
         s_pool = [sb.tile([P, U], F32, name=f"s_pool{u}") for u in range(2)]
         word_pool = sb.tile([P, T], I32, name="word_pool", align_bytes=64)
         byte_pool = sb.tile([P, T], U8, name="byte_pool")
-        w_raw = [sb.tile([P, PACK, D // 2], F32, name=f"w_raw{h}", align_bytes=64) for h in range(2)]
+        w_raw = sb.tile([P, PACK, D], F32, name="w_raw", align_bytes=64)
         query_raw = sb.tile([P, PACK, Q], F32, name="query_raw", align_bytes=64)
         qrot_raw = sb.tile([P, PACK, Q], F32, name="qrot_raw", align_bytes=64)
         lat_bytes = sb.tile([P, I], U8, name="lat_bytes", align_bytes=64)
@@ -61,10 +62,11 @@ def tile_attend_mla_expand_kernel(tc, lat_words, lat_scales, wuk, query, krot, c
             nc.sync.dma_start(lat_bytes[j:P:32, :].bitcast(I32), picked_bytes[8 * j : P : 32, :].bitcast(I32))
         nc.sync.dma_start(k_pool[2][:], k_rows[:, 2, :])
         nc.sync.dma_start(k_pool[3][:], k_rows[:, 3, :])
-        for h in range(2):
-            nc.sync.dma_start(w_raw[h][:], wuk.rearrange("(p j) d -> p j d", j=PACK)[:, :, h * D // 2 : (h + 1) * D // 2])
+        nc.sync.dma_start(w_raw[:], wuk.rearrange("(p j) d -> p j d", j=PACK))
         nc.sync.dma_start(word_pool[:], lat_words[0].rearrange("p n t -> p (n t)").bitcast(I32))
-        nc.sync.dma_start(query_raw[:], query.rearrange("(p j) q -> p j q", j=PACK))
+        query_dealt = query.rearrange("(n a r b) q -> r n a (b q)", a=2, r=2, b=2)
+        for r in range(2):
+            nc.sync.dma_start(query_raw[r:P:2].rearrange("n (a b) q -> n a (b q)", b=2), query_dealt[r])
         nc.sync.dma_start(qrot_raw[:], qrot.rearrange("(p j) q -> p j q", j=PACK))
 
         def quantise(name, grouped, width, tag=None):
@@ -118,15 +120,17 @@ def tile_attend_mla_expand_kernel(tc, lat_words, lat_scales, wuk, query, krot, c
                     ALU.add,
                 )
 
-        w_grouped = sb.tile([P, PACK, P, PACK], BF16, name="w_grouped", align_bytes=64)
-        for h in range(2):
-            nc.scalar.copy(
-                w_grouped[:, :, h * P // 2 : (h + 1) * P // 2, :].rearrange("p t m j -> p m j t"),
-                w_raw[h][:].rearrange("p j (m t) -> p m j t", t=PACK),
-            )
-        w_codes, w_scales = quantise("w", w_grouped[:].rearrange("p t m j -> p (t m j)"), D)
+        w_dealt = w_raw[:].rearrange("p j (n a r b) -> p a n j r b", a=2, r=2, b=2)
+        w_grouped = [sb.tile([P, 2, P, PACK], BF16, name=f"w_grouped{a}", align_bytes=64) for a in range(2)]
+        w_walk = [tile[:].rearrange("p b (n r) j -> p n j r b", r=2) for tile in w_grouped]
+        nc.scalar.copy(w_walk[0], w_dealt[:, 0])
+        nc.vector.tensor_copy(w_walk[1][:, W_SPLIT:], w_dealt[:, 1, W_SPLIT:])
+        nc.scalar.copy(w_walk[1][:, :W_SPLIT], w_dealt[:, 1, :W_SPLIT])
+        w_quantised = [
+            quantise(f"w{a}", grouped[:].rearrange("p b m j -> p (b m j)"), D // 2) for a, grouped in enumerate(w_grouped)
+        ]
 
-        km_grouped = sb.tile([P, I * PACK], BF16, name="km_grouped", tag="w_raw1", align_bytes=64)
+        km_grouped = sb.tile([P, I * PACK], BF16, name="km_grouped", tag="w_raw", align_bytes=64)
         for h, cols in enumerate(halves):
             nc.scalar.copy(
                 km_grouped[:, PACK * cols.start : PACK * cols.stop].bitcast(F32).rearrange("p (c i u) -> p c u i", i=RUN, u=2),
@@ -150,7 +154,8 @@ def tile_attend_mla_expand_kernel(tc, lat_words, lat_scales, wuk, query, krot, c
         for n, cols in enumerate(chunks):
             bank = ps.tile([P, PACK, CHUNK], F32, name=f"b_bank{n}")
             for t in range(PACK):
-                rows = slice(t * P, (t + 1) * P)
+                w_codes, w_scales = w_quantised[t // 2]
+                rows = slice(t % 2 * P, (t % 2 + 1) * P)
                 nc.tensor.matmul_mx(
                     out=bank[:, t, :],
                     lhsT=w_codes[:, rows].bitcast(FP8X4),

@@ -21,7 +21,7 @@ PACK = 4
 CHUNK = 128
 HALF = I // 2
 RUN = 4
-W_SPLIT = 32
+W_SPLIT = 16
 
 
 def tile_attend_mla_expand_kernel(tc, lat_words, lat_scales, wuk, query, krot, cosn, sinn, qrot, offs, offs2, out):
@@ -92,25 +92,32 @@ def tile_attend_mla_expand_kernel(tc, lat_words, lat_scales, wuk, query, krot, c
 
         pairs = [sb.tile([P, 2, HALF, 2], BF16, name=f"pairs{h}", align_bytes=64) for h in range(2)]
         for u in range(2):
-            gather_trig = gather_on_vector if u == 0 else gather_on_scalar
+            gather_sines = gather_on_vector if u == 0 else gather_on_scalar
             trig = sb.tile([P, 3, I], F32, name=f"trig{u}")
-            gather_trig(trig[:, 1, :], c_pool[u], places[:])
-            gather_trig(trig[:, 2, :], s_pool[u], places[:])
+            gather_on_vector(trig[:, 1, :], c_pool[u], places[:])
+            gather_sines(trig[:, 2, :], s_pool[u], places[:])
             nc.scalar.activation(trig[:, 0, :], trig[:, 2, :], ACT.Copy, scale=-1.0)
-            first = sb.tile([P, I], F32, name=f"first{u}")
-            second = [sb.tile([P, HALF], F32, name=f"second{u}_{h}") for h in range(2)]
-            for h, cols in enumerate(halves):
-                gather = gather_on_vector if (u, h) == (1, 0) else gather_on_scalar
-                gather(first[:, cols], k_pool[2 * u], listed(tokens, cols))
+            first = [sb.tile([P, HALF], F32, name=f"first{u}_{h}") for h in range(2)]
             prod_first = sb.tile([P, 2, I], F32, name=f"prod_first{u}")
-            nc.vector.tensor_tensor(prod_first[:], first[:].unsqueeze(1).to_broadcast([P, 2, I]), trig[:, 1:3, :], ALU.mult)
-            prod_second = [sb.tile([P, 2, HALF], F32, name=f"prod_second{u}_{h}") for h in range(2)]
             for h, cols in enumerate(halves):
-                gather = gather_on_vector if (u, h) == (1, 1) else gather_on_scalar
-                gather(second[h][:], k_pool[2 * u + 1], listed(tokens, cols))
+                gather_on_scalar(first[h][:], k_pool[2 * u], listed(tokens, cols))
             for h, cols in enumerate(halves):
                 nc.vector.tensor_tensor(
-                    prod_second[h][:], second[h][:].unsqueeze(1).to_broadcast([P, 2, HALF]), trig[:, 0:2, cols], ALU.mult
+                    prod_first[:, :, cols], first[h][:].unsqueeze(1).to_broadcast([P, 2, HALF]), trig[:, 1:3, cols], ALU.mult
+                )
+            prod_second = [sb.tile([P, 2, HALF], F32, name=f"prod_second{u}_{h}") for h in range(2)]
+            parts = [chunks[1], chunks[0], halves[1]] if u == 1 else halves
+            second = [sb.tile([P, cols.stop - cols.start], F32, name=f"second{u}_{n}") for n, cols in enumerate(parts)]
+            for n, cols in enumerate(parts):
+                gather = gather_on_vector if (u, n) == (1, 1) else gather_on_scalar
+                gather(second[n][:], k_pool[2 * u + 1], listed(tokens, cols))
+            for n, cols in enumerate(parts):
+                width = cols.stop - cols.start
+                nc.vector.tensor_tensor(
+                    prod_second[cols.start // HALF][:, :, cols.start % HALF : cols.start % HALF + width],
+                    second[n][:].unsqueeze(1).to_broadcast([P, 2, width]),
+                    trig[:, 0:2, cols],
+                    ALU.mult,
                 )
             for h, cols in enumerate(halves):
                 nc.vector.tensor_tensor(
@@ -123,9 +130,9 @@ def tile_attend_mla_expand_kernel(tc, lat_words, lat_scales, wuk, query, krot, c
         w_dealt = w_raw[:].rearrange("p j (n a r b) -> p a n j r b", a=2, r=2, b=2)
         w_grouped = [sb.tile([P, 2, P, PACK], BF16, name=f"w_grouped{a}", align_bytes=64) for a in range(2)]
         w_walk = [tile[:].rearrange("p b (n r) j -> p n j r b", r=2) for tile in w_grouped]
+        nc.scalar.copy(w_walk[1][:, :W_SPLIT], w_dealt[:, 1, :W_SPLIT])
         nc.scalar.copy(w_walk[0], w_dealt[:, 0])
         nc.vector.tensor_copy(w_walk[1][:, W_SPLIT:], w_dealt[:, 1, W_SPLIT:])
-        nc.scalar.copy(w_walk[1][:, :W_SPLIT], w_dealt[:, 1, :W_SPLIT])
         w_quantised = [
             quantise(f"w{a}", grouped[:].rearrange("p b m j -> p (b m j)"), D // 2) for a, grouped in enumerate(w_grouped)
         ]

@@ -22,6 +22,7 @@ CHUNK = 128
 HALF = I // 2
 RUN = 4
 W_SPLIT = 16
+LINE = 256
 
 
 def tile_attend_mla_expand_kernel(tc, lat_words, lat_scales, wuk, query, krot, cosn, sinn, qrot, offs, offs2, out):
@@ -30,34 +31,32 @@ def tile_attend_mla_expand_kernel(tc, lat_words, lat_scales, wuk, query, krot, c
         sb = ctx.enter_context(tc.tile_pool(name="sb", bufs=1))
         ps = ctx.enter_context(tc.psum_pool(name="ps", bufs=1))
 
-        tokens = sb.tile([P, I // 16], U16, name="tokens")
-        places = sb.tile([P, I // 16], U16, name="places")
+        tokens = sb.tile([P, I // 16], U16, name="tokens", align_bytes=LINE)
+        places = sb.tile([P, I // 16], U16, name="places", align_bytes=LINE)
         k_rows = krot.rearrange("(p t) n -> p t n", t=PACK)
-        c_rows = cosn.rearrange("(p t) n -> p t n", t=PACK)
-        s_rows = sinn.rearrange("(p t) n -> p t n", t=PACK)
-        k_pool = [sb.tile([P, T], F32, name=f"k_pool{t}") for t in range(PACK)]
-        c_pool = [sb.tile([P, U], F32, name=f"c_pool{u}") for u in range(2)]
-        s_pool = [sb.tile([P, U], F32, name=f"s_pool{u}") for u in range(2)]
-        word_pool = sb.tile([P, T], I32, name="word_pool", align_bytes=64)
-        byte_pool = sb.tile([P, T], U8, name="byte_pool")
-        w_raw = sb.tile([P, PACK, D], F32, name="w_raw", align_bytes=64)
-        query_raw = sb.tile([P, PACK, Q], F32, name="query_raw", align_bytes=64)
-        qrot_raw = sb.tile([P, PACK, Q], F32, name="qrot_raw", align_bytes=64)
-        lat_bytes = sb.tile([P, I], U8, name="lat_bytes", align_bytes=64)
-        picked_bytes = sb.tile([P, I], U8, name="picked_bytes")
+        c_rows = cosn.rearrange("(p t) n -> p (t n)", t=PACK)[:, U : 3 * U]
+        s_rows = sinn.rearrange("(p t) n -> p (t n)", t=PACK)[:, U : 3 * U]
+        k_pool = [sb.tile([P, T], F32, name=f"k_pool{t}", align_bytes=LINE) for t in range(PACK)]
+        c_pool = sb.tile([P, 2 * U], F32, name="c_pool", align_bytes=LINE)
+        s_pool = sb.tile([P, 2 * U], F32, name="s_pool", align_bytes=LINE)
+        word_pool = sb.tile([P, T], I32, name="word_pool", align_bytes=LINE)
+        byte_pool = sb.tile([P, T], U8, name="byte_pool", align_bytes=LINE)
+        w_raw = sb.tile([P, PACK, D], F32, name="w_raw", align_bytes=LINE)
+        query_raw = sb.tile([P, PACK, Q], F32, name="query_raw", align_bytes=LINE)
+        qrot_raw = sb.tile([P, PACK, Q], F32, name="qrot_raw", align_bytes=LINE)
+        lat_bytes = sb.tile([P, I], U8, name="lat_bytes", align_bytes=LINE)
+        picked_bytes = sb.tile([P, I], U8, name="picked_bytes", align_bytes=LINE)
         nc.vector.memset(byte_pool[:].bitcast(I32), 0)
         nc.vector.memset(lat_bytes[:].bitcast(I32), 0)
 
-        nc.sync.dma_start(c_pool[0][:], c_rows[:, 0, :])
+        nc.sync.dma_start(c_pool[:], c_rows)
         nc.sync.dma_start(places[:], offs2)
         nc.sync.dma_start(tokens[:], offs)
         nc.sync.dma_start(byte_pool[0:P:8, :].bitcast(I32), lat_scales[0].bitcast(I32))
-        nc.sync.dma_start(s_pool[0][:], s_rows[:, 0, :])
+        nc.sync.dma_start(s_pool[:], s_rows)
         nc.sync.dma_start(k_pool[0][:], k_rows[:, 0, :])
         nc.sync.dma_start(k_pool[1][:], k_rows[:, 1, :])
-        nc.sync.dma_start(c_pool[1][:], c_rows[:, 2, :])
         nc.vector.tensor_copy(picked_bytes[:], byte_pool[:].indirect(tokens[:]))
-        nc.sync.dma_start(s_pool[1][:], s_rows[:, 2, :])
         for j in range(4):
             nc.sync.dma_start(lat_bytes[j:P:32, :].bitcast(I32), picked_bytes[8 * j : P : 32, :].bitcast(I32))
         nc.sync.dma_start(k_pool[2][:], k_rows[:, 2, :])
@@ -70,8 +69,8 @@ def tile_attend_mla_expand_kernel(tc, lat_words, lat_scales, wuk, query, krot, c
         nc.sync.dma_start(qrot_raw[:], qrot.rearrange("(p j) q -> p j q", j=PACK))
 
         def quantise(name, grouped, width, tag=None):
-            codes = sb.tile([P, width], U32, name=f"{name}_codes", tag=tag or f"{name}_codes", align_bytes=64)
-            scales = sb.tile([P, width], U8, name=f"{name}_scales", align_bytes=64)
+            codes = sb.tile([P, width], U32, name=f"{name}_codes", tag=tag or f"{name}_codes", align_bytes=LINE)
+            scales = sb.tile([P, width], U8, name=f"{name}_scales", align_bytes=LINE)
             nc.vector.quantize_mx(out=codes[:].bitcast(FP8X4), scales=scales[:], in_=grouped)
             return codes, scales
 
@@ -82,25 +81,25 @@ def tile_attend_mla_expand_kernel(tc, lat_words, lat_scales, wuk, query, krot, c
             return offsets[:, cols.start // 16 : cols.stop // 16]
 
         def gather_on_scalar(picked, pool, offsets):
-            nc.scalar.activation(picked, pool[:].indirect(offsets), ACT.Copy)
+            nc.scalar.activation(picked, pool.indirect(offsets), ACT.Copy)
 
         def in_runs(view):
             return view.rearrange("p e (c i) -> p c e i", i=RUN)
 
         def gather_on_vector(picked, pool, offsets):
-            nc.vector.tensor_copy(picked, pool[:].indirect(offsets))
+            nc.vector.tensor_copy(picked, pool.indirect(offsets))
 
-        pairs = [sb.tile([P, 2, HALF, 2], BF16, name=f"pairs{h}", align_bytes=64) for h in range(2)]
-        for u in range(2):
-            gather_sines = gather_on_vector if u == 0 else gather_on_scalar
-            trig = sb.tile([P, 3, I], F32, name=f"trig{u}")
-            gather_on_vector(trig[:, 1, :], c_pool[u], places[:])
-            gather_sines(trig[:, 2, :], s_pool[u], places[:])
+        pairs = [sb.tile([P, 2, HALF, 2], BF16, name=f"pairs{h}", align_bytes=LINE) for h in range(2)]
+        trigs = [sb.tile([P, 3, I], F32, name=f"trig{u}") for u in range(2)]
+        for place, pool in ((1, c_pool), (2, s_pool)):
+            gather_on_scalar(trigs[0][:, place, :], pool[:], places[:])
+            gather_on_vector(trigs[1][:, place, :], pool[:, U:], places[:])
+        for u, trig in enumerate(trigs):
             nc.scalar.activation(trig[:, 0, :], trig[:, 2, :], ACT.Copy, scale=-1.0)
             first = [sb.tile([P, HALF], F32, name=f"first{u}_{h}") for h in range(2)]
             prod_first = sb.tile([P, 2, I], F32, name=f"prod_first{u}")
             for h, cols in enumerate(halves):
-                gather_on_scalar(first[h][:], k_pool[2 * u], listed(tokens, cols))
+                gather_on_scalar(first[h][:], k_pool[2 * u][:], listed(tokens, cols))
             for h, cols in enumerate(halves):
                 nc.vector.tensor_tensor(
                     prod_first[:, :, cols], first[h][:].unsqueeze(1).to_broadcast([P, 2, HALF]), trig[:, 1:3, cols], ALU.mult
@@ -110,7 +109,7 @@ def tile_attend_mla_expand_kernel(tc, lat_words, lat_scales, wuk, query, krot, c
             second = [sb.tile([P, cols.stop - cols.start], F32, name=f"second{u}_{n}") for n, cols in enumerate(parts)]
             for n, cols in enumerate(parts):
                 gather = gather_on_vector if (u, n) == (1, 1) else gather_on_scalar
-                gather(second[n][:], k_pool[2 * u + 1], listed(tokens, cols))
+                gather(second[n][:], k_pool[2 * u + 1][:], listed(tokens, cols))
             for n, cols in enumerate(parts):
                 width = cols.stop - cols.start
                 nc.vector.tensor_tensor(
@@ -128,7 +127,7 @@ def tile_attend_mla_expand_kernel(tc, lat_words, lat_scales, wuk, query, krot, c
                 )
 
         w_dealt = w_raw[:].rearrange("p j (n a r b) -> p a n j r b", a=2, r=2, b=2)
-        w_grouped = [sb.tile([P, 2, P, PACK], BF16, name=f"w_grouped{a}", align_bytes=64) for a in range(2)]
+        w_grouped = [sb.tile([P, 2, P, PACK], BF16, name=f"w_grouped{a}", align_bytes=LINE) for a in range(2)]
         w_walk = [tile[:].rearrange("p b (n r) j -> p n j r b", r=2) for tile in w_grouped]
         nc.scalar.copy(w_walk[1][:, :W_SPLIT], w_dealt[:, 1, :W_SPLIT])
         nc.scalar.copy(w_walk[0], w_dealt[:, 0])
@@ -137,27 +136,27 @@ def tile_attend_mla_expand_kernel(tc, lat_words, lat_scales, wuk, query, krot, c
             quantise(f"w{a}", grouped[:].rearrange("p b m j -> p (b m j)"), D // 2) for a, grouped in enumerate(w_grouped)
         ]
 
-        km_grouped = sb.tile([P, I * PACK], BF16, name="km_grouped", tag="w_raw", align_bytes=64)
+        km_grouped = sb.tile([P, I * PACK], BF16, name="km_grouped", tag="w_raw", align_bytes=LINE)
         for h, cols in enumerate(halves):
             nc.scalar.copy(
                 km_grouped[:, PACK * cols.start : PACK * cols.stop].bitcast(F32).rearrange("p (c i u) -> p c u i", i=RUN, u=2),
                 pairs[h][:].rearrange("p u i e -> p u (i e)").bitcast(F32).rearrange("p u (c i) -> p c u i", i=RUN),
             )
 
-        q_grouped = sb.tile([P, 2, Q, PACK], BF16, name="q_grouped", align_bytes=64)
+        q_grouped = sb.tile([P, 2, Q, PACK], BF16, name="q_grouped", align_bytes=LINE)
         for n, raw in enumerate((query_raw, qrot_raw)):
             nc.scalar.copy(
                 q_grouped[:, n].rearrange("p (c i) j -> p c j i", i=RUN),
                 raw[:].rearrange("p j (c i) -> p c j i", i=RUN),
             )
 
-        lat_codes = [sb.tile([P, CHUNK], U32, name=f"lat_codes{n}", align_bytes=64) for n in range(len(chunks))]
+        lat_codes = [sb.tile([P, CHUNK], U32, name=f"lat_codes{n}", align_bytes=LINE) for n in range(len(chunks))]
         for n, cols in enumerate(chunks):
             nc.vector.tensor_copy(lat_codes[n][:], word_pool[:].bitcast(U32).indirect(listed(tokens, cols)))
         km_codes, km_scales = quantise("km", km_grouped[:], I, tag="query_raw")
         q_codes, q_scales = quantise("q", q_grouped[:].rearrange("p n q j -> p (n q j)"), 2 * Q)
 
-        b_grouped = sb.tile([P, I * PACK], BF16, name="b_grouped", tag="qrot_raw", align_bytes=64)
+        b_grouped = sb.tile([P, I * PACK], BF16, name="b_grouped", tag="qrot_raw", align_bytes=LINE)
         for n, cols in enumerate(chunks):
             bank = ps.tile([P, PACK, CHUNK], F32, name=f"b_bank{n}")
             for t in range(PACK):
@@ -212,6 +211,6 @@ def tile_attend_mla_expand_kernel(tc, lat_words, lat_scales, wuk, query, krot, c
         nc.scalar.activation(weights[:], negated[:], ACT.Exp, bias=shift[:], scale=-1.0, accum_out=total[:])
         inverse = sb.tile([P, 1], F32, name="inverse")
         nc.vector.reciprocal(inverse[:], total[:])
-        result = sb.tile([P, I], F32, name="result")
+        result = sb.tile([P, I], F32, name="result", align_bytes=LINE)
         nc.vector.tensor_scalar(result[:], weights[:], inverse[:], float(I), ALU.mult, ALU.mult)
         nc.sync.dma_start(out, result[:])

@@ -57,10 +57,15 @@ def tile_attend_mla_expand_kernel(tc, lat_words, lat_scales, wuk, query, krot, c
         nc.sync.dma_start(k_pool[0][:], k_rows[:, 0, :])
         nc.sync.dma_start(k_pool[1][:], k_rows[:, 1, :])
         nc.vector.tensor_copy(picked_bytes[:], byte_pool[:].indirect(tokens[:]))
-        for j in range(4):
-            nc.sync.dma_start(lat_bytes[j:P:32, :].bitcast(I32), picked_bytes[8 * j : P : 32, :].bitcast(I32))
+
+        def move_scale_rows(cols):
+            for j in range(4):
+                nc.sync.dma_start(lat_bytes[j:P:32, cols].bitcast(I32), picked_bytes[8 * j : P : 32, cols].bitcast(I32))
+
+        move_scale_rows(slice(0, HALF))
         nc.sync.dma_start(k_pool[2][:], k_rows[:, 2, :])
         nc.sync.dma_start(k_pool[3][:], k_rows[:, 3, :])
+        move_scale_rows(slice(HALF, I))
         nc.sync.dma_start(w_raw[:], wuk.rearrange("(p j) d -> p j d", j=PACK))
         nc.sync.dma_start(word_pool[:], lat_words[0].rearrange("p n t -> p (n t)").bitcast(I32))
         query_dealt = query.rearrange("(n a r b) q -> r n a (b q)", a=2, r=2, b=2)

from contextlib import ExitStack

import concourse.mybir as mybir

C, D, R, T, I, U, Q = 512, 512, 512, 2048, 512, 1024, 128
FLOPS = 2 * C * D * I + 2 * (D + R) * Q * I

F32 = mybir.dt.float32
BF16 = mybir.dt.bfloat16
I32 = mybir.dt.int32
U32 = mybir.dt.uint32
U16 = mybir.dt.uint16
U8 = mybir.dt.uint8
FP8X4 = mybir.dt.float8_e4m3fn_x4
ALU = mybir.AluOpType
ACT = mybir.ActivationFunctionType
AXIS = mybir.AxisListType

P = 128
PACK = 4
CHUNK = 128
HALF = I // 2
RUN = 4
W_SPLIT = 16
LINE = 256


def tile_attend_mla_expand_kernel(tc, lat_words, lat_scales, wuk, query, krot, cosn, sinn, qrot, offs, offs2, out):
    nc = tc.nc
    with ExitStack() as ctx:
        sb = ctx.enter_context(tc.tile_pool(name="sb", bufs=1))
        ps = ctx.enter_context(tc.psum_pool(name="ps", bufs=1))

        tokens = sb.tile([P, I // 16], U16, name="tokens", align_bytes=LINE)
        places = sb.tile([P, I // 16], U16, name="places", align_bytes=LINE)
        k_rows = krot.rearrange("(p t) n -> p t n", t=PACK)
        c_rows = cosn.rearrange("(p t) n -> p (t n)", t=PACK)[:, U : 3 * U]
        s_rows = sinn.rearrange("(p t) n -> p (t n)", t=PACK)[:, U : 3 * U]
        k_pool = [sb.tile([P, T], F32, name=f"k_pool{t}", align_bytes=LINE) for t in range(PACK)]
        c_pool = sb.tile([P, 2 * U], F32, name="c_pool", align_bytes=LINE)
        s_pool = sb.tile([P, 2 * U], F32, name="s_pool", align_bytes=LINE)
        word_pool = sb.tile([P, T], I32, name="word_pool", align_bytes=LINE)
        byte_pool = sb.tile([P, T], U8, name="byte_pool", align_bytes=LINE)
        w_raw = sb.tile([P, PACK, D], F32, name="w_raw", align_bytes=LINE)
        query_raw = sb.tile([P, PACK, Q], F32, name="query_raw", align_bytes=LINE)
        qrot_raw = sb.tile([P, PACK, Q], F32, name="qrot_raw", align_bytes=LINE)
        lat_bytes = sb.tile([P, I], U8, name="lat_bytes", align_bytes=LINE)
        picked_bytes = sb.tile([P, I], U8, name="picked_bytes", align_bytes=LINE)
        nc.vector.memset(byte_pool[:].bitcast(I32), 0)
        nc.vector.memset(lat_bytes[:].bitcast(I32), 0)

        nc.sync.dma_start(c_pool[:], c_rows)
        nc.sync.dma_start(places[:], offs2)
        nc.sync.dma_start(tokens[:], offs)
        nc.sync.dma_start(byte_pool[0:P:8, :].bitcast(I32), lat_scales[0].bitcast(I32))
        nc.sync.dma_start(s_pool[:], s_rows)
        nc.sync.dma_start(k_pool[0][:], k_rows[:, 0, :])
        nc.sync.dma_start(k_pool[1][:], k_rows[:, 1, :])
        nc.vector.tensor_copy(picked_bytes[:], byte_pool[:].indirect(tokens[:]))

        def move_scale_rows(cols):
            for j in range(4):
                nc.sync.dma_start(lat_bytes[j:P:32, cols].bitcast(I32), picked_bytes[8 * j : P : 32, cols].bitcast(I32))

        move_scale_rows(slice(0, HALF))
        nc.sync.dma_start(k_pool[2][:], k_rows[:, 2, :])
        nc.sync.dma_start(k_pool[3][:], k_rows[:, 3, :])
        move_scale_rows(slice(HALF, I))
        nc.sync.dma_start(w_raw[:], wuk.rearrange("(p j) d -> p j d", j=PACK))
        nc.sync.dma_start(word_pool[:], lat_words[0].rearrange("p n t -> p (n t)").bitcast(I32))
        query_dealt = query.rearrange("(n a r b) q -> r n a (b q)", a=2, r=2, b=2)
        for r in range(2):
            nc.sync.dma_start(query_raw[r:P:2].rearrange("n (a b) q -> n a (b q)", b=2), query_dealt[r])
        nc.sync.dma_start(qrot_raw[:], qrot.rearrange("(p j) q -> p j q", j=PACK))

        def quantise(name, grouped, width, tag=None):
            codes = sb.tile([P, width], U32, name=f"{name}_codes", tag=tag or f"{name}_codes", align_bytes=LINE)
            scales = sb.tile([P, width], U8, name=f"{name}_scales", align_bytes=LINE)
            nc.vector.quantize_mx(out=codes[:].bitcast(FP8X4), scales=scales[:], in_=grouped)
            return codes, scales

        halves = [slice(h * HALF, (h + 1) * HALF) for h in range(2)]
        chunks = [slice(n * CHUNK, (n + 1) * CHUNK) for n in range(I // CHUNK)]

        def listed(offsets, cols):
            return offsets[:, cols.start // 16 : cols.stop // 16]

        def gather_on_scalar(picked, pool, offsets):
            nc.scalar.activation(picked, pool.indirect(offsets), ACT.Copy)

        def in_runs(view):
            return view.rearrange("p e (c i) -> p c e i", i=RUN)

        def gather_on_vector(picked, pool, offsets):
            nc.vector.tensor_copy(picked, pool.indirect(offsets))

        pairs = [sb.tile([P, 2, HALF, 2], BF16, name=f"pairs{h}", align_bytes=LINE) for h in range(2)]
        trigs = [sb.tile([P, 3, I], F32, name=f"trig{u}") for u in range(2)]
        for place, pool in ((1, c_pool), (2, s_pool)):
            gather_on_scalar(trigs[0][:, place, :], pool[:], places[:])
            gather_on_vector(trigs[1][:, place, :], pool[:, U:], places[:])
        for u, trig in enumerate(trigs):
            nc.scalar.activation(trig[:, 0, :], trig[:, 2, :], ACT.Copy, scale=-1.0)
            first = [sb.tile([P, HALF], F32, name=f"first{u}_{h}") for h in range(2)]
            prod_first = sb.tile([P, 2, I], F32, name=f"prod_first{u}")
            for h, cols in enumerate(halves):
                gather_on_scalar(first[h][:], k_pool[2 * u][:], listed(tokens, cols))
            for h, cols in enumerate(halves):
                nc.vector.tensor_tensor(
                    prod_first[:, :, cols], first[h][:].unsqueeze(1).to_broadcast([P, 2, HALF]), trig[:, 1:3, cols], ALU.mult
                )
            prod_second = [sb.tile([P, 2, HALF], F32, name=f"prod_second{u}_{h}") for h in range(2)]
            parts = [chunks[1], chunks[0], halves[1]] if u == 1 else halves
            second = [sb.tile([P, cols.stop - cols.start], F32, name=f"second{u}_{n}") for n, cols in enumerate(parts)]
            for n, cols in enumerate(parts):
                gather = gather_on_vector if (u, n) == (1, 1) else gather_on_scalar
                gather(second[n][:], k_pool[2 * u + 1][:], listed(tokens, cols))
            for n, cols in enumerate(parts):
                width = cols.stop - cols.start
                nc.vector.tensor_tensor(
                    prod_second[cols.start // HALF][:, :, cols.start % HALF : cols.start % HALF + width],
                    second[n][:].unsqueeze(1).to_broadcast([P, 2, width]),
                    trig[:, 0:2, cols],
                    ALU.mult,
                )
            for h, cols in enumerate(halves):
                nc.vector.tensor_tensor(
                    pairs[h][:, u].rearrange("p (c i) e -> p c e i", i=RUN),
                    in_runs(prod_first[:, :, cols]),
                    in_runs(prod_second[h][:]),
                    ALU.add,
                )

        w_dealt = w_raw[:].rearrange("p j (n a r b) -> p a n j r b", a=2, r=2, b=2)
        w_grouped = [sb.tile([P, 2, P, PACK], BF16, name=f"w_grouped{a}", align_bytes=LINE) for a in range(2)]
        w_walk = [tile[:].rearrange("p b (n r) j -> p n j r b", r=2) for tile in w_grouped]
        nc.scalar.copy(w_walk[1][:, :W_SPLIT], w_dealt[:, 1, :W_SPLIT])
        nc.scalar.copy(w_walk[0], w_dealt[:, 0])
        nc.vector.tensor_copy(w_walk[1][:, W_SPLIT:], w_dealt[:, 1, W_SPLIT:])
        w_quantised = [
            quantise(f"w{a}", grouped[:].rearrange("p b m j -> p (b m j)"), D // 2) for a, grouped in enumerate(w_grouped)
        ]

        km_grouped = sb.tile([P, I * PACK], BF16, name="km_grouped", tag="w_raw", align_bytes=LINE)
        for h, cols in enumerate(halves):
            nc.scalar.copy(
                km_grouped[:, PACK * cols.start : PACK * cols.stop].bitcast(F32).rearrange("p (c i u) -> p c u i", i=RUN, u=2),
                pairs[h][:].rearrange("p u i e -> p u (i e)").bitcast(F32).rearrange("p u (c i) -> p c u i", i=RUN),
            )

        q_grouped = sb.tile([P, 2, Q, PACK], BF16, name="q_grouped", align_bytes=LINE)
        for n, raw in enumerate((query_raw, qrot_raw)):
            nc.scalar.copy(
                q_grouped[:, n].rearrange("p (c i) j -> p c j i", i=RUN),
                raw[:].rearrange("p j (c i) -> p c j i", i=RUN),
            )

        lat_codes = [sb.tile([P, CHUNK], U32, name=f"lat_codes{n}", align_bytes=LINE) for n in range(len(chunks))]
        for n, cols in enumerate(chunks):
            nc.vector.tensor_copy(lat_codes[n][:], word_pool[:].bitcast(U32).indirect(listed(tokens, cols)))
        km_codes, km_scales = quantise("km", km_grouped[:], I, tag="query_raw")
        q_codes, q_scales = quantise("q", q_grouped[:].rearrange("p n q j -> p (n q j)"), 2 * Q)

        b_grouped = sb.tile([P, I * PACK], BF16, name="b_grouped", tag="qrot_raw", align_bytes=LINE)
        for n, cols in enumerate(chunks):
            bank = ps.tile([P, PACK, CHUNK], F32, name=f"b_bank{n}")
            for t in range(PACK):
                w_codes, w_scales = w_quantised[t // 2]
                rows = slice(t % 2 * P, (t % 2 + 1) * P)
                nc.tensor.matmul_mx(
                    out=bank[:, t, :],
                    lhsT=w_codes[:, rows].bitcast(FP8X4),
                    lhsT_scale=w_scales[:, rows],
                    rhs=lat_codes[n][:].bitcast(FP8X4),
                    rhs_scale=lat_bytes[:, cols],
                    start=True,
                    stop=True,
                )
            copy = nc.vector.tensor_copy if n == 2 else nc.scalar.copy
            copy(
                b_grouped[:, PACK * cols.start : PACK * cols.stop].rearrange("p (c i t) -> p c t i", i=2, t=PACK),
                bank[:].rearrange("p t (c i) -> p c t i", i=2),
            )

        early = ps.tile([P, I - CHUNK], F32, name="scores_early", tag="b_bank1")
        last = ps.tile([P, CHUNK], F32, name="scores_last", tag="b_bank2")
        for n, cols in enumerate(chunks):
            b_codes, b_scales = quantise(f"b{n}", b_grouped[:, PACK * cols.start : PACK * cols.stop], CHUNK)
            scores = last[:] if n == 3 else early[:, cols]
            nc.tensor.matmul_mx(
                out=scores,
                lhsT=q_codes[:, Q:].bitcast(FP8X4),
                lhsT_scale=q_scales[:, Q:],
                rhs=km_codes[:, cols].bitcast(FP8X4),
                rhs_scale=km_scales[:, cols],
                start=True,
                stop=False,
            )
            nc.tensor.matmul_mx(
                out=scores,
                lhsT=q_codes[:, :Q].bitcast(FP8X4),
                lhsT_scale=q_scales[:, :Q],
                rhs=b_codes[:].bitcast(FP8X4),
                rhs_scale=b_scales[:],
                start=False,
                stop=True,
            )
        negated = sb.tile([P, I], F32, name="negated")
        start_value = None
        for n, (scores, cols) in enumerate(((early, slice(0, I - CHUNK)), (last, chunks[3]))):
            shift = sb.tile([P, 1], F32, name=f"shift{n}")
            nc.vector.tensor_scalar(negated[:, cols], scores[:], -1.0, start_value, ALU.mult, ALU.min, accum_out=shift[:])
            start_value = shift[:]
        weights = sb.tile([P, I], F32, name="weights")
        total = sb.tile([P, 1], F32, name="total")
        nc.scalar.activation(weights[:], negated[:], ACT.Exp, bias=shift[:], scale=-1.0, accum_out=total[:])
        inverse = sb.tile([P, 1], F32, name="inverse")
        nc.vector.reciprocal(inverse[:], total[:])
        result = sb.tile([P, I], F32, name="result", align_bytes=LINE)
        nc.vector.tensor_scalar(result[:], weights[:], inverse[:], float(I), ALU.mult, ALU.mult)
        nc.sync.dma_start(out, result[:])
